import numpy as np
import ml_dtypes


def mxq(x, axis, fmt="e4m3"):
    dtype, down = {"e4m3": (ml_dtypes.float8_e4m3fn, 7), "e5m2": (ml_dtypes.float8_e5m2, 14)}[fmt]
    v = np.moveaxis(np.asarray(x, np.float32).astype(ml_dtypes.bfloat16).astype(np.float64), axis, -1)
    blocks = v.reshape(v.shape[:-1] + (-1, 32))
    amax = np.abs(blocks).max(-1, keepdims=True)
    byte = np.maximum(np.where(amax > 0, np.frexp(amax)[1] - 1 + 127, 0) - down, 1)
    scale = np.exp2(byte - 127.0)
    codes = (blocks / scale).astype(np.float32).astype(dtype).astype(np.float64)
    return np.moveaxis((codes * scale).reshape(v.shape), -1, axis)


WIDE = False


def mx_kscale(k):
    if not WIDE:
        return np.ones(k)
    levels = np.array([10, -10, 5, -5, 0])
    if k % 512:
        return np.exp2(np.random.permutation(np.resize(levels, k // 32))).repeat(32)
    a = np.empty((k // 512, 16))
    for p in range(k // 512):
        a[p, :8] = np.random.permutation(np.resize(levels, 8))
        for g in range(8):
            far = levels[np.abs(levels - a[p, g]) >= 10]
            a[p, g + 8] = far[np.random.randint(len(far))]
    return np.exp2(a.ravel()).repeat(32)


def f64(x):
    return np.asarray(x).astype(np.float64)


def striped(idx):
    return np.tile(idx.reshape(-1, 16).T, (8, 1)).astype(np.uint16)


def unstriped(offs):
    return offs[:16].T.reshape(-1).astype(np.int64)


E2M1 = np.array([0.0, 0.5, 1.0, 1.5, 2.0, 3.0, 4.0, 6.0, -0.0, -0.5, -1.0, -1.5, -2.0, -3.0, -4.0, -6.0])


def pack_weight(w, fmt):
    k, n = w.shape
    w = f64(np.asarray(w, np.float32).astype(ml_dtypes.bfloat16)).reshape(k // 32, 32, n)
    amax = np.abs(w).max(1)
    if fmt == "e4m3":
        byte = np.frexp(amax)[1] - 1 + 127 - 7
    else:
        mant, ex = np.frexp(amax / 6.0)
        byte = np.where(mant > 0.5, ex, ex - 1) + 127
    byte = np.clip(np.where(amax > 0, byte, 1), 1, 254)
    scaled = (w * np.exp2(127.0 - byte)[:, None, :]).reshape(k, n).astype(np.float32)
    by_word = np.ascontiguousarray(scaled.reshape(k // 512, 128, 4, n).transpose(0, 1, 3, 2))
    if fmt == "e4m3":
        words = by_word.astype(ml_dtypes.float8_e4m3fn).view(np.uint8)
    else:
        c = by_word.astype(ml_dtypes.float4_e2m1fn).view(np.uint8) & 0xF
        words = (c[..., 0::2] | (c[..., 1::2] << 4)).reshape(k // 512, 128, 2 * n)
    return np.ascontiguousarray(words), np.ascontiguousarray(byte.astype(np.uint8).reshape(k // 512, 16, n))


def unpack_weight(words, scales, fmt):
    g, _, n = scales.shape
    words = np.ascontiguousarray(words).reshape(g, 128, n, -1)
    if fmt == "e4m3":
        vals = words.view(ml_dtypes.float8_e4m3fn).astype(np.float64)
    else:
        nib = np.empty((g, 128, n, 4), np.uint8)
        nib[..., 0::2] = words & 0xF
        nib[..., 1::2] = words >> 4
        vals = E2M1[nib]
    vals = vals * np.repeat(np.exp2(scales.astype(np.float64) - 127.0), 8, axis=1)[..., None]
    return vals.transpose(0, 1, 3, 2).reshape(g * 512, n)


def gelu(v):
    return 0.5 * v * (1.0 + np.tanh(np.sqrt(2.0 / np.pi) * (v + 0.044715 * v**3)))


K, H, N, T, S, T2 = 1536, 1024, 512, 4096, 1024, 2048

def setup_inputs():
    n = np.random.standard_normal
    s = mx_kscale(K)[:, None]
    u = mx_kscale(H)[:, None]
    tab_words, tab_scales = pack_weight(n((K, T)) * s, "e4m3")
    w1 = (n((K, H)) / np.sqrt(K) / s * u.T).astype(np.float32)
    w2_words, w2_scales = pack_weight(n((H, N)) * np.sqrt(2.0 / H) / u, "e2m1")
    offs = striped(np.random.permutation(T)[:S])
    offs2 = striped(np.random.permutation(T2)[:S])
    wgo = np.exp(0.3 * n((128, S))).astype(np.float32)
    return {"tab_words": tab_words, "tab_scales": tab_scales, "w1": w1,
            "w2_words": w2_words, "w2_scales": w2_scales,
            "offs": offs, "offs2": offs2, "wgo": wgo}

def reference(tab_words, tab_scales, w1, w2_words, w2_scales, offs, offs2, wgo):
    v = unpack_weight(tab_words, tab_scales, "e4m3")[:, unstriped(offs)]
    w2 = unpack_weight(w2_words, w2_scales, "e2m1")
    h = np.maximum(mxq(f64(w1), 0, "e4m3").T @ v, 0.0)
    z = w2.T @ mxq(h, 0, "e4m3")
    y = z / np.sqrt(np.abs(z) + 0.1)
    out = np.zeros((N, T2))
    out[:, unstriped(offs2)] = np.tile(f64(wgo), (N // 128, 1)) * y
    return out

@@ -1,0 +1,219 @@
+from contextlib import ExitStack
+
+import concourse.mybir as mybir
+
+K, H, N, T, S, T2 = 1536, 1024, 512, 4096, 1024, 2048
+FLOPS = 2 * K * H * S + 2 * H * N * S
+
+F32 = mybir.dt.float32
+BF16 = mybir.dt.bfloat16
+I32 = mybir.dt.int32
+U32 = mybir.dt.uint32
+U16 = mybir.dt.uint16
+U8 = mybir.dt.uint8
+FP8X4 = mybir.dt.float8_e4m3fn_x4
+FP4X4 = mybir.dt.float4_e2m1fn_x4
+ACT = mybir.ActivationFunctionType
+MULT = mybir.AluOpType.mult
+
+P = 128
+PACK = 4
+K_PASS = P * PACK
+KP = K // K_PASS
+HP = H // K_PASS
+NT = N // P
+BLK = 128
+WHOLE = ((0, 512),)
+LOAD_CUTS = {(0, 0): WHOLE, (0, 1): WHOLE, (0, 2): WHOLE, (1, 0): WHOLE, (1, 1): WHOLE, (1, 2): ((0, 256), (256, 512))}
+HALF = (("v", 0, 64), ("s", 64, 128))
+ALL = (("v", 0, 128),)
+CAST_CUTS = {(0, 0): HALF, (0, 1): HALF, (0, 2): HALF, (1, 0): ALL, (1, 1): ALL, (1, 2): (("v", 0, 64), ("v", 64, 128))}
+EPS = 0.1
+
+
+def tile_list_descriptor_power_compression_kernel(tc, tab_words, tab_scales, w1, w2_words, w2_scales, offs, offs2, wgo, out):
+    nc = tc.nc
+    with ExitStack() as ctx:
+        keep = ctx.enter_context(tc.tile_pool(name="keep", bufs=1))
+        ring = ctx.enter_context(tc.tile_pool(name="ring", bufs=3))
+        psum = ctx.enter_context(tc.psum_pool(name="psum", bufs=1))
+
+        hits = keep.tile([P, S // 16], U16, name="hits")
+        places = keep.tile([P, S // 16], U16, name="places")
+        nc.sync.dma_start(hits[:], offs)
+
+        warm_in = keep.tile([P, 1], F32, name="warm_in")
+        warm_out = keep.tile([P, 1], F32, name="warm_out")
+        nc.vector.memset(warm_in[:], 1.0)
+        nc.scalar.activation(warm_out[:], warm_in[:], ACT.Abs_reciprocal_sqrt)
+
+        tab_sc = keep.tile([P, T // 4], I32, name="tab_sc", align_bytes=64)
+        nc.gpsimd.memset(tab_sc[:], 0)
+        w2_sc = keep.tile([P, HP * N // 4], I32, name="w2_sc", align_bytes=64)
+
+        for a in range(KP):
+            for q in range(4):
+                nc.gpsimd.dma_start(tab_sc[32 * q + 4 * a : 32 * q + 4 * a + 4, :], tab_scales[a, 4 * q : 4 * q + 4, :].bitcast(I32))
+
+        nc.gpsimd.memset(w2_sc[:], 0)
+
+        tab = []
+        raw = {}
+        for g in range(HP):
+            for a in range(KP):
+                if g == 0:
+                    words = keep.tile([P, T], I32, name=f"tab{a}", align_bytes=64)
+                    nc.sync.dma_start(words[:], tab_words[a].rearrange("p t i -> p (t i)").bitcast(I32))
+                    tab.append(words)
+                chunk = keep.tile([P, PACK, K_PASS], F32, name=f"raw{g}{a}")
+                rows = w1[a * K_PASS : (a + 1) * K_PASS, g * K_PASS : (g + 1) * K_PASS].rearrange("(p j) c -> p j c", j=PACK)
+                for c0, c1 in LOAD_CUTS[g, a]:
+                    nc.sync.dma_start(chunk[:, :, c0:c1], rows[:, :, c0:c1])
+                raw[g, a] = chunk
+        nc.sync.dma_start(places[:], offs2)
+
+        for q in range(4):
+            nc.sync.dma_start(
+                w2_sc[32 * q : 32 * q + 4, :].rearrange("r (a c) -> r a c", a=HP),
+                w2_scales[:, 4 * q : 4 * q + 4, :].rearrange("a r c -> r a c").bitcast(I32),
+            )
+        w2_codes = keep.tile([P, HP, 2 * N // 4], I32, name="w2_codes", align_bytes=64)
+        nc.sync.dma_start(w2_codes[:], w2_words.rearrange("a p c -> p a c").bitcast(I32))
+        weight = keep.tile([P, S], F32, name="weight")
+        nc.sync.dma_start(weight[:], wgo)
+
+        cache = []
+        for n in range(NT):
+            window = keep.tile([P, T2], F32, name=f"cache{n}")
+            nc.gpsimd.memset(window[:], 0.0)
+            cache.append(window)
+
+        v_codes = []
+        for a in range(KP):
+            picked = keep.tile([P, S], U32, name=f"v_codes{a}", align_bytes=64)
+            nc.vector.tensor_copy(picked[:], tab[a][:].bitcast(U32).indirect(hits[:]))
+            v_codes.append(picked)
+        v_sc = keep.tile([P, S], U8, name="v_sc", align_bytes=64)
+        nc.vector.tensor_copy(v_sc[:], tab_sc[:].bitcast(U8).indirect(hits[:]))
+
+        w1_codes = {}
+        w1_sc = {}
+        for g in range(HP):
+            for a in range(KP):
+                grouped = ring.tile([P, PACK, P, PACK], BF16, name="grouped", align_bytes=64)
+                dst = grouped[:].rearrange("p t m j -> p m j t")
+                src = raw[g, a][:].rearrange("p j (m t) -> p m j t", t=PACK)
+                for who, m0, m1 in CAST_CUTS[g, a]:
+                    if who == "v":
+                        nc.vector.tensor_copy(dst[:, m0:m1], src[:, m0:m1])
+                    else:
+                        nc.scalar.copy(dst[:, m0:m1], src[:, m0:m1])
+                codes = keep.tile([P, K_PASS], U32, name=f"w1_codes{g}{a}", align_bytes=64)
+                scales = keep.tile([P, K_PASS], U8, name=f"w1_sc{g}{a}", align_bytes=64)
+                if (g, a) == (HP - 1, KP - 1):
+                    for t in range(PACK):
+                        cols = slice(t * P, (t + 1) * P)
+                        nc.vector.quantize_mx(out=codes[:, cols].bitcast(FP8X4), scales=scales[:, cols], in_=grouped[:, t].rearrange("p m j -> p (m j)"))
+                else:
+                    nc.vector.quantize_mx(out=codes[:].bitcast(FP8X4), scales=scales[:], in_=grouped[:].rearrange("p t m j -> p (t m j)"))
+                w1_codes[g, a] = codes
+                w1_sc[g, a] = scales
+
+        h_codes = [keep.tile([P, S], U32, name=f"h_codes{g}", align_bytes=64) for g in range(HP)]
+        h_sc = [keep.tile([P, S], U8, name=f"h_sc{g}", align_bytes=64) for g in range(HP)]
+        w2_sc_bytes = w2_sc[:].bitcast(U8)
+
+        def sums(g, blocks, accs, passes):
+            for a in passes:
+                for b0 in range(0, len(blocks), 2):
+                    for t in range(PACK):
+                        for b in blocks[b0 : b0 + 2]:
+                            cols = slice(b * BLK, (b + 1) * BLK)
+                            nc.tensor.matmul_mx(
+                                out=accs[b][:, t, :],
+                                lhsT=w1_codes[g, a][:, t * P : (t + 1) * P].bitcast(FP8X4),
+                                lhsT_scale=w1_sc[g, a][:, t * P : (t + 1) * P],
+                                rhs=v_codes[a][:, cols].bitcast(FP8X4),
+                                rhs_scale=v_sc[4 * a : P, cols],
+                                start=(a == 0 and t == 0),
+                                stop=(a == KP - 1 and t == PACK - 1),
+                            )
+
+        def hidden(g, pair, accs, first):
+            relu = ring.tile([P, 2 * BLK, PACK], BF16, name="relu", align_bytes=64)
+            for i, b in enumerate(pair):
+                part = relu[:, i * BLK : (i + 1) * BLK, :]
+                if first and i == 1:
+                    nc.vector.tensor_scalar_max(part, accs[b][:].rearrange("p t n -> p n t"), 0.0)
+                else:
+                    nc.scalar.activation(part, accs[b][:].rearrange("p t n -> p n t"), ACT.Relu)
+            if first:
+                for i, b in enumerate(pair):
+                    cols = slice(b * BLK, (b + 1) * BLK)
+                    part = relu[:, i * BLK : (i + 1) * BLK, :]
+                    nc.vector.quantize_mx(out=h_codes[g][:, cols].bitcast(FP8X4), scales=h_sc[g][:, cols], in_=part.rearrange("p n t -> p (n t)"))
+            else:
+                cols = slice(pair[0] * BLK, (pair[1] + 1) * BLK)
+                nc.vector.quantize_mx(out=h_codes[g][:, cols].bitcast(FP8X4), scales=h_sc[g][:, cols], in_=relu[:].rearrange("p n t -> p (n t)"))
+
+        def banks(blocks, first_bank):
+            return {b: psum.tile([P, PACK, BLK], F32, name=f"bank{first_bank + i}") for i, b in enumerate(blocks)}
+
+        def project(n, tok0, width, bank):
+            z = psum.tile([P, width], F32, name=f"bank{bank}")
+            step = width if width == 512 else BLK
+            for c0 in range(0, width, step):
+                cols = slice(tok0 + c0, tok0 + c0 + step)
+                for g in range(HP):
+                    nc.tensor.matmul_mx(
+                        out=z[:, c0 : c0 + step],
+                        lhsT=w2_codes[:, g, n * (P // 2) : (n + 1) * (P // 2)].bitcast(U8).bitcast(FP4X4),
+                        lhsT_scale=w2_sc_bytes[:, g * N + n * P : g * N + (n + 1) * P],
+                        rhs=h_codes[g][:, cols].bitcast(FP8X4),
+                        rhs_scale=h_sc[g][:, cols],
+                        start=(g == 0),
+                        stop=(g == HP - 1),
+                    )
+            size = ring.tile([P, width], F32, name="size")
+            nc.scalar.activation(size[:], z[:], ACT.Abs)
+            inv = ring.tile([P, width], F32, name="inv")
+            nc.scalar.activation(inv[:], size[:], ACT.Abs_reciprocal_sqrt, bias=EPS)
+            y = ring.tile([P, width], F32, name="y")
+            nc.vector.tensor_tensor(y[:], z[:], inv[:], MULT)
+            return y
+
+        def put(n, tok0, width, y):
+            where = places[:, tok0 // 16 : (tok0 + width) // 16]
+            nc.vector.tensor_tensor(cache[n][:].indirect(where), y[:], weight[:, tok0 : tok0 + width], MULT)
+            if tok0 + width == S:
+                nc.sync.dma_start(out[n * P : (n + 1) * P, :], cache[n][:])
+
+        pending = []
+
+        def finish(tok0, width, first_bank):
+            for n in range(NT):
+                y = project(n, tok0, width, first_bank + n)
+                if pending:
+                    put(*pending.pop())
+                pending.append((n, tok0, width, y))
+
+        every = list(range(S // BLK))
+        accs = banks(every, 0)
+        sums(0, every, accs, range(KP))
+        for b in range(0, len(every), 2):
+            hidden(0, every[b : b + 2], accs, False)
+
+        early, late = every[:4], every[4:]
+        accs = banks(early, 0)
+        sums(1, early, accs, range(KP))
+        hidden(1, early[:2], accs, True)
+        finish(0, 256, 4)
+        hidden(1, early[2:], accs, False)
+        accs = banks(late, 0)
+        for b in range(0, len(late), 2):
+            sums(1, late[b : b + 2], accs, range(KP))
+        finish(256, 256, 4)
+        for b in range(0, len(late), 2):
+            hidden(1, late[b : b + 2], accs, False)
+        finish(512, 512, 0)
+        put(*pending.pop())

@@ -41,6 +41,7 @@ def tile_list_descriptor_power_compression_kernel(tc, tab_words, tab_scales, w1,
         hits = keep.tile([P, S // 16], U16, name="hits")
         places = keep.tile([P, S // 16], U16, name="places")
         nc.sync.dma_start(hits[:], offs)
+        nc.sync.dma_start(places[:], offs2)
 
         warm_in = keep.tile([P, 1], F32, name="warm_in")
         warm_out = keep.tile([P, 1], F32, name="warm_out")
@@ -48,14 +49,15 @@ def tile_list_descriptor_power_compression_kernel(tc, tab_words, tab_scales, w1,
         nc.scalar.activation(warm_out[:], warm_in[:], ACT.Abs_reciprocal_sqrt)
 
         tab_sc = keep.tile([P, T // 4], I32, name="tab_sc", align_bytes=64)
-        nc.gpsimd.memset(tab_sc[:], 0)
+        nc.vector.memset(tab_sc[:], 0)
         w2_sc = keep.tile([P, HP * N // 4], I32, name="w2_sc", align_bytes=64)
 
         for a in range(KP):
             for q in range(4):
-                nc.gpsimd.dma_start(tab_sc[32 * q + 4 * a : 32 * q + 4 * a + 4, :], tab_scales[a, 4 * q : 4 * q + 4, :].bitcast(I32))
+                queue = nc.gpsimd if a < KP - 1 else nc.scalar
+                queue.dma_start(tab_sc[32 * q + 4 * a : 32 * q + 4 * a + 4, :], tab_scales[a, 4 * q : 4 * q + 4, :].bitcast(I32))
 
-        nc.gpsimd.memset(w2_sc[:], 0)
+        nc.vector.memset(w2_sc[:], 0)
 
         tab = []
         raw = {}
@@ -70,7 +72,6 @@ def tile_list_descriptor_power_compression_kernel(tc, tab_words, tab_scales, w1,
                 for c0, c1 in LOAD_CUTS[g, a]:
                     nc.sync.dma_start(chunk[:, :, c0:c1], rows[:, :, c0:c1])
                 raw[g, a] = chunk
-        nc.sync.dma_start(places[:], offs2)
 
         for q in range(4):
             nc.sync.dma_start(
@@ -85,7 +86,7 @@ def tile_list_descriptor_power_compression_kernel(tc, tab_words, tab_scales, w1,
         cache = []
         for n in range(NT):
             window = keep.tile([P, T2], F32, name=f"cache{n}")
-            nc.gpsimd.memset(window[:], 0.0)
+            nc.vector.memset(window[:], 0.0)
             cache.append(window)
 
         v_codes = []

@@ -24,10 +24,10 @@ HP = H // K_PASS
 NT = N // P
 BLK = 128
 WHOLE = ((0, 512),)
-LOAD_CUTS = {(0, 0): WHOLE, (0, 1): WHOLE, (0, 2): WHOLE, (1, 0): WHOLE, (1, 1): WHOLE, (1, 2): ((0, 256), (256, 512))}
+HALVES = ((0, 256), (256, 512))
+LOAD_CUTS = {(0, 0): WHOLE, (0, 1): WHOLE, (0, 2): WHOLE, (1, 0): HALVES, (1, 1): WHOLE, (1, 2): HALVES}
 HALF = (("v", 0, 64), ("s", 64, 128))
-ALL = (("v", 0, 128),)
-CAST_CUTS = {(0, 0): HALF, (0, 1): HALF, (0, 2): HALF, (1, 0): ALL, (1, 1): ALL, (1, 2): (("v", 0, 64), ("v", 64, 128))}
+CAST_CUTS = {(0, 0): HALF, (0, 1): HALF, (0, 2): HALF, (1, 0): (("s", 0, 64), ("v", 64, 128)), (1, 1): (("v", 0, 96), ("s", 96, 128)), (1, 2): (("v", 0, 64), ("v", 64, 128))}
 EPS = 0.1
 
 
@@ -45,28 +45,27 @@ def tile_list_descriptor_power_compression_kernel(tc, tab_words, tab_scales, w1,
 
         warm_in = keep.tile([P, 1], F32, name="warm_in")
         warm_out = keep.tile([P, 1], F32, name="warm_out")
-        nc.vector.memset(warm_in[:], 1.0)
+        nc.gpsimd.memset(warm_in[:], 1.0)
         nc.scalar.activation(warm_out[:], warm_in[:], ACT.Abs_reciprocal_sqrt)
 
         tab_sc = keep.tile([P, T // 4], I32, name="tab_sc", align_bytes=64)
         nc.vector.memset(tab_sc[:], 0)
         w2_sc = keep.tile([P, HP * N // 4], I32, name="w2_sc", align_bytes=64)
 
-        for a in range(KP):
-            for q in range(4):
-                queue = nc.gpsimd if a < KP - 1 else nc.scalar
-                queue.dma_start(tab_sc[32 * q + 4 * a : 32 * q + 4 * a + 4, :], tab_scales[a, 4 * q : 4 * q + 4, :].bitcast(I32))
+        tab = [keep.tile([P, T], I32, name=f"tab{a}", align_bytes=64) for a in range(KP)]
+        words = [tab_words[a].rearrange("p t i -> p (t i)").bitcast(I32) for a in range(KP)]
+        for c0 in range(0, T, T // 4):
+            nc.sync.dma_start(tab[0][:, c0 : c0 + T // 4], words[0][:, c0 : c0 + T // 4])
+        for q in range(4):
+            nc.sync.dma_start(tab_sc[32 * q : 32 * q + 4 * KP, :], tab_scales[:, 4 * q : 4 * q + 4, :].bitcast(I32))
 
         nc.vector.memset(w2_sc[:], 0)
 
-        tab = []
         raw = {}
         for g in range(HP):
             for a in range(KP):
-                if g == 0:
-                    words = keep.tile([P, T], I32, name=f"tab{a}", align_bytes=64)
-                    nc.sync.dma_start(words[:], tab_words[a].rearrange("p t i -> p (t i)").bitcast(I32))
-                    tab.append(words)
+                if g == 0 and a > 0:
+                    nc.sync.dma_start(tab[a][:], words[a])
                 chunk = keep.tile([P, PACK, K_PASS], F32, name=f"raw{g}{a}")
                 rows = w1[a * K_PASS : (a + 1) * K_PASS, g * K_PASS : (g + 1) * K_PASS].rearrange("(p j) c -> p j c", j=PACK)
                 for c0, c1 in LOAD_CUTS[g, a]:
@@ -102,13 +101,14 @@ def tile_list_descriptor_power_compression_kernel(tc, tab_words, tab_scales, w1,
         for g in range(HP):
             for a in range(KP):
                 grouped = ring.tile([P, PACK, P, PACK], BF16, name="grouped", align_bytes=64)
-                dst = grouped[:].rearrange("p t m j -> p m j t")
-                src = raw[g, a][:].rearrange("p j (m t) -> p m j t", t=PACK)
+                dst = grouped[:].rearrange("p (u e) m j -> p u m j e", e=2)
+                src = raw[g, a][:].rearrange("p j (m u e) -> p u m j e", u=2, e=2)
                 for who, m0, m1 in CAST_CUTS[g, a]:
                     if who == "v":
-                        nc.vector.tensor_copy(dst[:, m0:m1], src[:, m0:m1])
+                        nc.vector.tensor_copy(dst[:, :, m0:m1], src[:, :, m0:m1])
                     else:
-                        nc.scalar.copy(dst[:, m0:m1], src[:, m0:m1])
+                        for u in range(2):
+                            nc.scalar.copy(dst[:, u, m0:m1], src[:, u, m0:m1])
                 codes = keep.tile([P, K_PASS], U32, name=f"w1_codes{g}{a}", align_bytes=64)
                 scales = keep.tile([P, K_PASS], U8, name=f"w1_sc{g}{a}", align_bytes=64)
                 if (g, a) == (HP - 1, KP - 1):
@@ -191,8 +191,8 @@ def tile_list_descriptor_power_compression_kernel(tc, tab_words, tab_scales, w1,
 
         pending = []
 
-        def finish(tok0, width, first_bank):
-            for n in range(NT):
+        def finish(tok0, width, rows, first_bank):
+            for n in rows:
                 y = project(n, tok0, width, first_bank + n)
                 if pending:
                     put(*pending.pop())
@@ -205,16 +205,15 @@ def tile_list_descriptor_power_compression_kernel(tc, tab_words, tab_scales, w1,
             hidden(0, every[b : b + 2], accs, False)
 
         early, late = every[:4], every[4:]
-        accs = banks(early, 0)
+        accs = banks(every, 0)
         sums(1, early, accs, range(KP))
         hidden(1, early[:2], accs, True)
-        finish(0, 256, 4)
+        finish(0, 256, (0, 1), 0)
         hidden(1, early[2:], accs, False)
-        accs = banks(late, 0)
-        for b in range(0, len(late), 2):
-            sums(1, late[b : b + 2], accs, range(KP))
-        finish(256, 256, 4)
+        finish(0, 256, (2, 3), 0)
+        sums(1, late, accs, range(KP))
         for b in range(0, len(late), 2):
             hidden(1, late[b : b + 2], accs, False)
-        finish(512, 512, 0)
+        finish(256, 256, range(NT), 4)
+        finish(512, 512, range(NT), 0)
         put(*pending.pop())

@@ -23,12 +23,6 @@ KP = K // K_PASS
 HP = H // K_PASS
 NT = N // P
 BLK = 128
-WHOLE = ((0, 512),)
-HALVES = ((0, 256), (256, 512))
-LOAD_CUTS = {(0, 0): WHOLE, (0, 1): WHOLE, (0, 2): WHOLE, (1, 0): HALVES, (1, 1): WHOLE, (1, 2): HALVES}
-HALF = (("v", 0, 64), ("s", 64, 128))
-CAST_CUTS = {(0, 0): HALF, (0, 1): HALF, (0, 2): HALF, (1, 0): (("s", 0, 64), ("v", 64, 128)), (1, 1): (("v", 0, 96), ("s", 96, 128)), (1, 2): (("v", 0, 64), ("v", 64, 128))}
-EPS = 0.1
 
 
 def tile_list_descriptor_power_compression_kernel(tc, tab_words, tab_scales, w1, w2_words, w2_scales, offs, offs2, wgo, out):
@@ -43,10 +37,10 @@ def tile_list_descriptor_power_compression_kernel(tc, tab_words, tab_scales, w1,
         nc.sync.dma_start(hits[:], offs)
         nc.sync.dma_start(places[:], offs2)
 
-        warm_in = keep.tile([P, 1], F32, name="warm_in")
-        warm_out = keep.tile([P, 1], F32, name="warm_out")
-        nc.gpsimd.memset(warm_in[:], 1.0)
-        nc.scalar.activation(warm_out[:], warm_in[:], ACT.Abs_reciprocal_sqrt)
+        hundred = keep.tile([P, 1], F32, name="hundred")
+        eps = keep.tile([P, 1], F32, name="eps")
+        nc.gpsimd.memset(hundred[:], 100.0)
+        nc.scalar.activation(eps[:], hundred[:], ACT.Abs_reciprocal_sqrt)
 
         tab_sc = keep.tile([P, T // 4], I32, name="tab_sc", align_bytes=64)
         nc.vector.memset(tab_sc[:], 0)
@@ -54,23 +48,21 @@ def tile_list_descriptor_power_compression_kernel(tc, tab_words, tab_scales, w1,
 
         tab = [keep.tile([P, T], I32, name=f"tab{a}", align_bytes=64) for a in range(KP)]
         words = [tab_words[a].rearrange("p t i -> p (t i)").bitcast(I32) for a in range(KP)]
-        for c0 in range(0, T, T // 4):
-            nc.sync.dma_start(tab[0][:, c0 : c0 + T // 4], words[0][:, c0 : c0 + T // 4])
+        raw = [keep.tile([P, PACK, H], F32, name=f"raw{a}") for a in range(KP - 1)]
+        rows = [w1[a * K_PASS : (a + 1) * K_PASS, :].rearrange("(p j) c -> p j c", j=PACK) for a in range(KP)]
+        for j in range(PACK):
+            nc.sync.dma_start(raw[0][:, j, :], rows[0][:, j, :])
         for q in range(4):
             nc.sync.dma_start(tab_sc[32 * q : 32 * q + 4 * KP, :], tab_scales[:, 4 * q : 4 * q + 4, :].bitcast(I32))
-
         nc.vector.memset(w2_sc[:], 0)
-
-        raw = {}
-        for g in range(HP):
-            for a in range(KP):
-                if g == 0 and a > 0:
-                    nc.sync.dma_start(tab[a][:], words[a])
-                chunk = keep.tile([P, PACK, K_PASS], F32, name=f"raw{g}{a}")
-                rows = w1[a * K_PASS : (a + 1) * K_PASS, g * K_PASS : (g + 1) * K_PASS].rearrange("(p j) c -> p j c", j=PACK)
-                for c0, c1 in LOAD_CUTS[g, a]:
-                    nc.sync.dma_start(chunk[:, :, c0:c1], rows[:, :, c0:c1])
-                raw[g, a] = chunk
+        nc.sync.dma_start(tab[0][:], words[0])
+        nc.sync.dma_start(raw[1][:], rows[1])
+        nc.sync.dma_start(tab[1][:], words[1])
+        nc.sync.dma_start(tab[2][:], words[2])
+        last = {}
+        for c0, c1 in ((0, 512), (512, 768), (768, 1024)):
+            last[c0] = keep.tile([P, PACK, c1 - c0], F32, name=f"last{c0}")
+            nc.sync.dma_start(last[c0][:], rows[2][:, :, c0:c1])
 
         for q in range(4):
             nc.sync.dma_start(
@@ -88,37 +80,45 @@ def tile_list_descriptor_power_compression_kernel(tc, tab_words, tab_scales, w1,
             nc.vector.memset(window[:], 0.0)
             cache.append(window)
 
-        v_codes = []
-        for a in range(KP):
-            picked = keep.tile([P, S], U32, name=f"v_codes{a}", align_bytes=64)
-            nc.vector.tensor_copy(picked[:], tab[a][:].bitcast(U32).indirect(hits[:]))
-            v_codes.append(picked)
         v_sc = keep.tile([P, S], U8, name="v_sc", align_bytes=64)
-        nc.vector.tensor_copy(v_sc[:], tab_sc[:].bitcast(U8).indirect(hits[:]))
-
+        v_codes = [keep.tile([P, S if a < KP - 1 else S // 2], U32, name=f"v_codes{a}", align_bytes=64) for a in range(KP)]
+        v_late = []
         w1_codes = {}
         w1_sc = {}
-        for g in range(HP):
-            for a in range(KP):
-                grouped = ring.tile([P, PACK, P, PACK], BF16, name="grouped", align_bytes=64)
-                dst = grouped[:].rearrange("p (u e) m j -> p u m j e", e=2)
-                src = raw[g, a][:].rearrange("p j (m u e) -> p u m j e", u=2, e=2)
-                for who, m0, m1 in CAST_CUTS[g, a]:
-                    if who == "v":
-                        nc.vector.tensor_copy(dst[:, :, m0:m1], src[:, :, m0:m1])
-                    else:
-                        for u in range(2):
-                            nc.scalar.copy(dst[:, u, m0:m1], src[:, u, m0:m1])
-                codes = keep.tile([P, K_PASS], U32, name=f"w1_codes{g}{a}", align_bytes=64)
-                scales = keep.tile([P, K_PASS], U8, name=f"w1_sc{g}{a}", align_bytes=64)
-                if (g, a) == (HP - 1, KP - 1):
-                    for t in range(PACK):
-                        cols = slice(t * P, (t + 1) * P)
-                        nc.vector.quantize_mx(out=codes[:, cols].bitcast(FP8X4), scales=scales[:, cols], in_=grouped[:, t].rearrange("p m j -> p (m j)"))
+
+        def gather(a):
+            nc.vector.tensor_copy(v_codes[a][:], tab[a][:].bitcast(U32).indirect(hits[:]))
+
+        def prepare(g, a, cuts, by_slice):
+            grouped = ring.tile([P, PACK, P, PACK], BF16, name="grouped", align_bytes=64)
+            dst = grouped[:].rearrange("p (u e) m j -> p u m j e", e=2)
+            codes = keep.tile([P, K_PASS], U32, name=f"w1_codes{g}{a}", align_bytes=64)
+            scales = keep.tile([P, K_PASS], U8, name=f"w1_sc{g}{a}", align_bytes=64)
+            for who, m0, m1, piece in cuts:
+                src = piece.rearrange("p j (m u e) -> p u m j e", u=2, e=2)
+                if who == "v":
+                    nc.vector.tensor_copy(dst[:, :, m0:m1], src)
                 else:
-                    nc.vector.quantize_mx(out=codes[:].bitcast(FP8X4), scales=scales[:], in_=grouped[:].rearrange("p t m j -> p (t m j)"))
-                w1_codes[g, a] = codes
-                w1_sc[g, a] = scales
+                    for u in range(2):
+                        nc.scalar.copy(dst[:, u, m0:m1], src[:, u])
+            if by_slice:
+                for t in range(PACK):
+                    cols = slice(t * P, (t + 1) * P)
+                    nc.vector.quantize_mx(out=codes[:, cols].bitcast(FP8X4), scales=scales[:, cols], in_=grouped[:, t].rearrange("p m j -> p (m j)"))
+            else:
+                nc.vector.quantize_mx(out=codes[:].bitcast(FP8X4), scales=scales[:], in_=grouped[:].rearrange("p t m j -> p (t m j)"))
+            w1_codes[g, a] = codes
+            w1_sc[g, a] = scales
+
+        nc.vector.tensor_copy(v_sc[:], tab_sc[:].bitcast(U8).indirect(hits[:]))
+        for a in range(KP - 1):
+            for g in range(HP):
+                prepare(g, a, (("s", 0, P, raw[a][:, :, g * K_PASS : (g + 1) * K_PASS]),), False)
+            gather(a)
+        half = S // 2
+        nc.vector.tensor_copy(v_codes[KP - 1][:], tab[KP - 1][:].bitcast(U32).indirect(hits[:, : half // 16]))
+        prepare(0, KP - 1, (("v", 0, 80, last[0][:, :, 0:320]), ("s", 80, P, last[0][:, :, 320:512])), False)
+        prepare(1, KP - 1, (("s", 0, 64, last[512][:]), ("v", 64, P, last[768][:])), True)
 
         h_codes = [keep.tile([P, S], U32, name=f"h_codes{g}", align_bytes=64) for g in range(HP)]
         h_sc = [keep.tile([P, S], U8, name=f"h_sc{g}", align_bytes=64) for g in range(HP)]
@@ -134,14 +134,17 @@ def tile_list_descriptor_power_compression_kernel(tc, tab_words, tab_scales, w1,
                                 out=accs[b][:, t, :],
                                 lhsT=w1_codes[g, a][:, t * P : (t + 1) * P].bitcast(FP8X4),
                                 lhsT_scale=w1_sc[g, a][:, t * P : (t + 1) * P],
-                                rhs=v_codes[a][:, cols].bitcast(FP8X4),
+                                rhs=(v_late[0][:, b * BLK - half : (b + 1) * BLK - half] if a == KP - 1 and b >= 4 else v_codes[a][:, cols]).bitcast(FP8X4),
                                 rhs_scale=v_sc[4 * a : P, cols],
                                 start=(a == 0 and t == 0),
                                 stop=(a == KP - 1 and t == PACK - 1),
                             )
 
-        def hidden(g, pair, accs, first):
-            relu = ring.tile([P, 2 * BLK, PACK], BF16, name="relu", align_bytes=64)
+        def hidden(g, pair, accs, first, slot=None):
+            if slot:
+                relu = keep.tile([P, 2 * BLK, PACK], BF16, name=slot, align_bytes=64)
+            else:
+                relu = ring.tile([P, 2 * BLK, PACK], BF16, name="relu", align_bytes=64)
             for i, b in enumerate(pair):
                 part = relu[:, i * BLK : (i + 1) * BLK, :]
                 if first and i == 1:
@@ -175,11 +178,17 @@ def tile_list_descriptor_power_compression_kernel(tc, tab_words, tab_scales, w1,
                         start=(g == 0),
                         stop=(g == HP - 1),
                     )
-            size = ring.tile([P, width], F32, name="size")
+            if tok0 == 0 and n < 2:
+                size = keep.tile([P, width], F32, name=f"slot_first{n}", align_bytes=64)
+            else:
+                size = ring.tile([P, width], F32, name="size")
             nc.scalar.activation(size[:], z[:], ACT.Abs)
             inv = ring.tile([P, width], F32, name="inv")
-            nc.scalar.activation(inv[:], size[:], ACT.Abs_reciprocal_sqrt, bias=EPS)
-            y = ring.tile([P, width], F32, name="y")
+            nc.scalar.activation(inv[:], size[:], ACT.Abs_reciprocal_sqrt, bias=eps[:])
+            if tok0 == 256 and n >= 2:
+                y = keep.tile([P, width], F32, name=f"slot_late{n - 2}", align_bytes=64)
+            else:
+                y = ring.tile([P, width], F32, name="y")
             nc.vector.tensor_tensor(y[:], z[:], inv[:], MULT)
             return y
 
@@ -191,29 +200,40 @@ def tile_list_descriptor_power_compression_kernel(tc, tab_words, tab_scales, w1,
 
         pending = []
 
-        def finish(tok0, width, rows, first_bank):
+        def finish(tok0, width, rows, z_banks):
             for n in rows:
-                y = project(n, tok0, width, first_bank + n)
+                y = project(n, tok0, width, z_banks[n])
                 if pending:
                     put(*pending.pop())
                 pending.append((n, tok0, width, y))
 
-        every = list(range(S // BLK))
-        accs = banks(every, 0)
-        sums(0, every, accs, range(KP))
-        for b in range(0, len(every), 2):
-            hidden(0, every[b : b + 2], accs, False)
+        accs = [banks((0, 1, 2, 3), 4 * g) for g in range(HP)]
+        for a in range(KP - 1):
+            for g in range(HP):
+                sums(g, [0, 1, 2, 3], accs[g], (a,))
+        sums(0, [0, 1], accs[0], (KP - 1,))
+        hidden(0, (0, 1), accs[0], False)
+        sums(0, [2, 3], accs[0], (KP - 1,))
+        sums(1, [0, 1], accs[1], (KP - 1,))
+        hidden(1, (0, 1), accs[1], True, "slot_gather")
+        v_late.append(keep.tile([P, half], U32, name="slot_gather", align_bytes=64))
+        nc.vector.tensor_copy(v_late[0][:], tab[KP - 1][:].bitcast(U32).indirect(hits[:, half // 16 :]))
+        sums(1, [2, 3], accs[1], (KP - 1,))
+        z_banks = (0, 1, 4, 5)
+        finish(0, 256, (0, 1), z_banks)
+        for g in range(HP):
+            hidden(g, (2, 3), accs[g], False, f"slot_first{g}")
+        finish(0, 256, (2, 3), z_banks)
 
-        early, late = every[:4], every[4:]
-        accs = banks(every, 0)
-        sums(1, early, accs, range(KP))
-        hidden(1, early[:2], accs, True)
-        finish(0, 256, (0, 1), 0)
-        hidden(1, early[2:], accs, False)
-        finish(0, 256, (2, 3), 0)
-        sums(1, late, accs, range(KP))
-        for b in range(0, len(late), 2):
-            hidden(1, late[b : b + 2], accs, False)
-        finish(256, 256, range(NT), 4)
-        finish(512, 512, range(NT), 0)
+        def later(pair, held):
+            for g in range(HP):
+                acc = banks(pair, 4 * g + 2)
+                sums(g, list(pair), acc, range(KP))
+                hidden(g, pair, acc, False, f"slot_late{g}" if held else None)
+
+        later((4, 5), False)
+        finish(256, 256, (0, 1), z_banks)
+        later((6, 7), True)
+        finish(256, 256, (2, 3), z_banks)
+        finish(512, 512, range(NT), z_banks)
         put(*pending.pop())

@@ -163,6 +163,9 @@ def tile_list_descriptor_power_compression_kernel(tc, tab_words, tab_scales, w1,
         def banks(blocks, first_bank):
             return {b: psum.tile([P, PACK, BLK], F32, name=f"bank{first_bank + i}") for i, b in enumerate(blocks)}
 
+        def fused(n, tok0):
+            return tok0 == 0 or (tok0 == 256 and n == 0)
+
         def project(n, tok0, width, bank):
             z = psum.tile([P, width], F32, name=f"bank{bank}")
             step = width if width == 512 else BLK
@@ -178,6 +181,12 @@ def tile_list_descriptor_power_compression_kernel(tc, tab_words, tab_scales, w1,
                         start=(g == 0),
                         stop=(g == HP - 1),
                     )
+            first = tok0 < S // 2
+            if not first:
+                plain = ring.tile([P, width], F32, name="plain")
+                nc.scalar.copy(plain[:], z[:])
+                weighted = ring.tile([P, width], F32, name="weighted")
+                nc.gpsimd.tensor_tensor(weighted[:], plain[:], weight[:, tok0 : tok0 + width], MULT)
             if tok0 == 0 and n < 2:
                 size = keep.tile([P, width], F32, name=f"slot_first{n}", align_bytes=64)
             else:
@@ -185,16 +194,27 @@ def tile_list_descriptor_power_compression_kernel(tc, tab_words, tab_scales, w1,
             nc.scalar.activation(size[:], z[:], ACT.Abs)
             inv = ring.tile([P, width], F32, name="inv")
             nc.scalar.activation(inv[:], size[:], ACT.Abs_reciprocal_sqrt, bias=eps[:])
-            if tok0 == 256 and n >= 2:
-                y = keep.tile([P, width], F32, name=f"slot_late{n - 2}", align_bytes=64)
+            if first:
+                if tok0 == 256 and n >= 2:
+                    bare = keep.tile([P, width], F32, name=f"slot_late{n - 2}", align_bytes=64)
+                else:
+                    bare = ring.tile([P, width], F32, name="bare")
+                nc.vector.tensor_tensor(bare[:], z[:], inv[:], MULT)
+                if fused(n, tok0):
+                    return bare
+            y = ring.tile([P, width], F32, name="y")
+            if first:
+                nc.gpsimd.tensor_tensor(y[:], bare[:], weight[:, tok0 : tok0 + width], MULT)
             else:
-                y = ring.tile([P, width], F32, name="y")
-            nc.vector.tensor_tensor(y[:], z[:], inv[:], MULT)
+                nc.gpsimd.tensor_tensor(y[:], weighted[:], inv[:], MULT)
             return y
 
         def put(n, tok0, width, y):
             where = places[:, tok0 // 16 : (tok0 + width) // 16]
-            nc.vector.tensor_tensor(cache[n][:].indirect(where), y[:], weight[:, tok0 : tok0 + width], MULT)
+            if fused(n, tok0):
+                nc.vector.tensor_tensor(cache[n][:].indirect(where), y[:], weight[:, tok0 : tok0 + width], MULT)
+            else:
+                nc.vector.tensor_copy(cache[n][:].indirect(where), y[:])
             if tok0 + width == S:
                 nc.sync.dma_start(out[n * P : (n + 1) * P, :], cache[n][:])
 
@@ -235,5 +255,7 @@ def tile_list_descriptor_power_compression_kernel(tc, tab_words, tab_scales, w1,
         finish(256, 256, (0, 1), z_banks)
         later((6, 7), True)
         finish(256, 256, (2, 3), z_banks)
-        finish(512, 512, range(NT), z_banks)
+        finish(512, 256, (0, 1), (1, 0))
+        finish(768, 256, (0, 1), (4, 5))
+        finish(512, 512, (2, 3), (0, 0, 0, 1))
         put(*pending.pop())

@@ -34,8 +34,6 @@ def tile_list_descriptor_power_compression_kernel(tc, tab_words, tab_scales, w1,
 
         hits = keep.tile([P, S // 16], U16, name="hits")
         places = keep.tile([P, S // 16], U16, name="places")
-        nc.sync.dma_start(hits[:], offs)
-        nc.sync.dma_start(places[:], offs2)
 
         hundred = keep.tile([P, 1], F32, name="hundred")
         eps = keep.tile([P, 1], F32, name="eps")
@@ -52,13 +50,15 @@ def tile_list_descriptor_power_compression_kernel(tc, tab_words, tab_scales, w1,
         rows = [w1[a * K_PASS : (a + 1) * K_PASS, :].rearrange("(p j) c -> p j c", j=PACK) for a in range(KP)]
         for j in range(PACK):
             nc.sync.dma_start(raw[0][:, j, :], rows[0][:, j, :])
+        nc.sync.dma_start(hits[:], offs)
+        nc.sync.dma_start(places[:], offs2)
         for q in range(4):
             nc.sync.dma_start(tab_sc[32 * q : 32 * q + 4 * KP, :], tab_scales[:, 4 * q : 4 * q + 4, :].bitcast(I32))
         nc.vector.memset(w2_sc[:], 0)
-        nc.sync.dma_start(tab[0][:], words[0])
-        nc.sync.dma_start(raw[1][:], rows[1])
-        nc.sync.dma_start(tab[1][:], words[1])
         nc.sync.dma_start(tab[2][:], words[2])
+        nc.sync.dma_start(raw[1][:], rows[1])
+        nc.sync.dma_start(tab[0][:], words[0])
+        nc.sync.dma_start(tab[1][:], words[1])
         last = {}
         for c0, c1 in ((0, 512), (512, 768), (768, 1024)):
             last[c0] = keep.tile([P, PACK, c1 - c0], F32, name=f"last{c0}")
@@ -81,8 +81,8 @@ def tile_list_descriptor_power_compression_kernel(tc, tab_words, tab_scales, w1,
             cache.append(window)
 
         v_sc = keep.tile([P, S], U8, name="v_sc", align_bytes=64)
-        v_codes = [keep.tile([P, S if a < KP - 1 else S // 2], U32, name=f"v_codes{a}", align_bytes=64) for a in range(KP)]
-        v_late = []
+        v_codes = [keep.tile([P, S if a == 2 else S // 2], U32, name=f"v_codes{a}", align_bytes=64) for a in range(KP)]
+        v_late = [keep.tile([P, S // 2], U32, name="v_late0", align_bytes=64)]
         w1_codes = {}
         w1_sc = {}
 
@@ -114,9 +114,11 @@ def tile_list_descriptor_power_compression_kernel(tc, tab_words, tab_scales, w1,
         for a in range(KP - 1):
             for g in range(HP):
                 prepare(g, a, (("s", 0, P, raw[a][:, :, g * K_PASS : (g + 1) * K_PASS]),), False)
-            gather(a)
         half = S // 2
-        nc.vector.tensor_copy(v_codes[KP - 1][:], tab[KP - 1][:].bitcast(U32).indirect(hits[:, : half // 16]))
+        gather(2)
+        nc.vector.tensor_copy(v_codes[0][:], tab[0][:].bitcast(U32).indirect(hits[:, : half // 16]))
+        nc.vector.tensor_copy(v_late[0][:], tab[0][:].bitcast(U32).indirect(hits[:, half // 16 :]))
+        nc.vector.tensor_copy(v_codes[1][:], tab[1][:].bitcast(U32).indirect(hits[:, : half // 16]))
         prepare(0, KP - 1, (("v", 0, 80, last[0][:, :, 0:320]), ("s", 80, P, last[0][:, :, 320:512])), False)
         prepare(1, KP - 1, (("s", 0, 64, last[512][:]), ("v", 64, P, last[768][:])), True)
 
@@ -134,7 +136,7 @@ def tile_list_descriptor_power_compression_kernel(tc, tab_words, tab_scales, w1,
                                 out=accs[b][:, t, :],
                                 lhsT=w1_codes[g, a][:, t * P : (t + 1) * P].bitcast(FP8X4),
                                 lhsT_scale=w1_sc[g, a][:, t * P : (t + 1) * P],
-                                rhs=(v_late[0][:, b * BLK - half : (b + 1) * BLK - half] if a == KP - 1 and b >= 4 else v_codes[a][:, cols]).bitcast(FP8X4),
+                                rhs=(v_late[a][:, b * BLK - half : (b + 1) * BLK - half] if a < 2 and b >= 4 else v_codes[a][:, cols]).bitcast(FP8X4),
                                 rhs_scale=v_sc[4 * a : P, cols],
                                 start=(a == 0 and t == 0),
                                 stop=(a == KP - 1 and t == PACK - 1),
@@ -163,69 +165,57 @@ def tile_list_descriptor_power_compression_kernel(tc, tab_words, tab_scales, w1,
         def banks(blocks, first_bank):
             return {b: psum.tile([P, PACK, BLK], F32, name=f"bank{first_bank + i}") for i, b in enumerate(blocks)}
 
-        def fused(n, tok0):
-            return tok0 == 0 or (tok0 == 256 and n == 0)
-
-        def project(n, tok0, width, bank):
-            z = psum.tile([P, width], F32, name=f"bank{bank}")
+        def project(rows, tok0, width, bank, how, slot=None, bare_slot=None):
+            shape = [P, len(rows), width]
+            z = psum.tile(shape, F32, name=f"bank{bank}")
             step = width if width == 512 else BLK
-            for c0 in range(0, width, step):
-                cols = slice(tok0 + c0, tok0 + c0 + step)
-                for g in range(HP):
-                    nc.tensor.matmul_mx(
-                        out=z[:, c0 : c0 + step],
-                        lhsT=w2_codes[:, g, n * (P // 2) : (n + 1) * (P // 2)].bitcast(U8).bitcast(FP4X4),
-                        lhsT_scale=w2_sc_bytes[:, g * N + n * P : g * N + (n + 1) * P],
-                        rhs=h_codes[g][:, cols].bitcast(FP8X4),
-                        rhs_scale=h_sc[g][:, cols],
-                        start=(g == 0),
-                        stop=(g == HP - 1),
-                    )
-            first = tok0 < S // 2
-            if not first:
-                plain = ring.tile([P, width], F32, name="plain")
-                nc.scalar.copy(plain[:], z[:])
-                weighted = ring.tile([P, width], F32, name="weighted")
-                nc.gpsimd.tensor_tensor(weighted[:], plain[:], weight[:, tok0 : tok0 + width], MULT)
-            if tok0 == 0 and n < 2:
-                size = keep.tile([P, width], F32, name=f"slot_first{n}", align_bytes=64)
+            for i, n in enumerate(rows):
+                for c0 in range(0, width, step):
+                    cols = slice(tok0 + c0, tok0 + c0 + step)
+                    for g in range(HP):
+                        nc.tensor.matmul_mx(
+                            out=z[:, i, c0 : c0 + step],
+                            lhsT=w2_codes[:, g, n * (P // 2) : (n + 1) * (P // 2)].bitcast(U8).bitcast(FP4X4),
+                            lhsT_scale=w2_sc_bytes[:, g * N + n * P : g * N + (n + 1) * P],
+                            rhs=h_codes[g][:, cols].bitcast(FP8X4),
+                            rhs_scale=h_sc[g][:, cols],
+                            start=(g == 0),
+                            stop=(g == HP - 1),
+                        )
+            factor = weight[:, tok0 : tok0 + width].unsqueeze(1).to_broadcast(shape)
+            if slot:
+                size = keep.tile(shape, F32, name=slot, align_bytes=64)
             else:
-                size = ring.tile([P, width], F32, name="size")
+                size = ring.tile(shape, F32, name="size")
             nc.scalar.activation(size[:], z[:], ACT.Abs)
-            inv = ring.tile([P, width], F32, name="inv")
+            if how == "gg":
+                plain = ring.tile(shape, F32, name="plain")
+                nc.scalar.copy(plain[:], z[:])
+                weighted = ring.tile(shape, F32, name="weighted")
+                nc.gpsimd.tensor_tensor(weighted[:], plain[:], factor, MULT)
+            inv = ring.tile(shape, F32, name="inv")
             nc.scalar.activation(inv[:], size[:], ACT.Abs_reciprocal_sqrt, bias=eps[:])
-            if first:
-                if tok0 == 256 and n >= 2:
-                    bare = keep.tile([P, width], F32, name=f"slot_late{n - 2}", align_bytes=64)
-                else:
-                    bare = ring.tile([P, width], F32, name="bare")
-                nc.vector.tensor_tensor(bare[:], z[:], inv[:], MULT)
-                if fused(n, tok0):
-                    return bare
-            y = ring.tile([P, width], F32, name="y")
-            if first:
-                nc.gpsimd.tensor_tensor(y[:], bare[:], weight[:, tok0 : tok0 + width], MULT)
-            else:
+            if how == "gg":
+                y = ring.tile(shape, F32, name="y")
                 nc.gpsimd.tensor_tensor(y[:], weighted[:], inv[:], MULT)
-            return y
-
-        def put(n, tok0, width, y):
-            where = places[:, tok0 // 16 : (tok0 + width) // 16]
-            if fused(n, tok0):
-                nc.vector.tensor_tensor(cache[n][:].indirect(where), y[:], weight[:, tok0 : tok0 + width], MULT)
             else:
-                nc.vector.tensor_copy(cache[n][:].indirect(where), y[:])
-            if tok0 + width == S:
-                nc.sync.dma_start(out[n * P : (n + 1) * P, :], cache[n][:])
-
-        pending = []
-
-        def finish(tok0, width, rows, z_banks):
-            for n in rows:
-                y = project(n, tok0, width, z_banks[n])
-                if pending:
-                    put(*pending.pop())
-                pending.append((n, tok0, width, y))
+                if bare_slot:
+                    bare = keep.tile(shape, F32, name=bare_slot, align_bytes=64)
+                else:
+                    bare = ring.tile(shape, F32, name="bare")
+                nc.vector.tensor_tensor(bare[:], z[:], inv[:], MULT)
+                y = bare
+                if how != "fused":
+                    y = ring.tile(shape, F32, name="y")
+                    (nc.vector if how == "vv" else nc.gpsimd).tensor_tensor(y[:], bare[:], factor, MULT)
+            for i, n in enumerate(rows):
+                where = places[:, tok0 // 16 : (tok0 + width) // 16]
+                if how == "fused":
+                    nc.vector.tensor_tensor(cache[n][:].indirect(where), y[:, i, :], weight[:, tok0 : tok0 + width], MULT)
+                else:
+                    nc.vector.tensor_copy(cache[n][:].indirect(where), y[:, i, :])
+                if tok0 + width == S:
+                    nc.sync.dma_start(out[n * P : (n + 1) * P, :], cache[n][:])
 
         accs = [banks((0, 1, 2, 3), 4 * g) for g in range(HP)]
         for a in range(KP - 1):
@@ -237,25 +227,29 @@ def tile_list_descriptor_power_compression_kernel(tc, tab_words, tab_scales, w1,
         sums(1, [0, 1], accs[1], (KP - 1,))
         hidden(1, (0, 1), accs[1], True, "slot_gather")
         v_late.append(keep.tile([P, half], U32, name="slot_gather", align_bytes=64))
-        nc.vector.tensor_copy(v_late[0][:], tab[KP - 1][:].bitcast(U32).indirect(hits[:, half // 16 :]))
+        nc.vector.tensor_copy(v_late[1][:], tab[1][:].bitcast(U32).indirect(hits[:, half // 16 :]))
         sums(1, [2, 3], accs[1], (KP - 1,))
-        z_banks = (0, 1, 4, 5)
-        finish(0, 256, (0, 1), z_banks)
+
+        def later(g, pair, first_bank, slot=None):
+            acc = banks(pair, first_bank)
+            sums(g, list(pair), acc, range(KP))
+            hidden(g, pair, acc, False, slot)
+
+        project((0,), 0, 256, 0, "fused", "slot_first0")
+        project((1,), 0, 256, 1, "fused", "slot_first1")
         for g in range(HP):
             hidden(g, (2, 3), accs[g], False, f"slot_first{g}")
-        finish(0, 256, (2, 3), z_banks)
-
-        def later(pair, held):
-            for g in range(HP):
-                acc = banks(pair, 4 * g + 2)
-                sums(g, list(pair), acc, range(KP))
-                hidden(g, pair, acc, False, f"slot_late{g}" if held else None)
-
-        later((4, 5), False)
-        finish(256, 256, (0, 1), z_banks)
-        later((6, 7), True)
-        finish(256, 256, (2, 3), z_banks)
-        finish(512, 256, (0, 1), (1, 0))
-        finish(768, 256, (0, 1), (4, 5))
-        finish(512, 512, (2, 3), (0, 0, 0, 1))
-        put(*pending.pop())
+        project((2,), 0, 256, 4, "fused")
+        project((3,), 0, 256, 5, "fused")
+        later(0, (4, 5), 2)
+        later(1, (4, 5), 6)
+        project((0,), 256, 256, 0, "fused")
+        project((1,), 256, 256, 1, "vg")
+        later(0, (6, 7), 2, "slot_late0")
+        later(1, (6, 7), 6, "slot_late1")
+        project((2,), 256, 256, 4, "vv", None, "slot_late0")
+        project((3,), 256, 256, 5, "vv", None, "slot_late1")
+        project((0, 1), 512, 256, 1, "gg")
+        project((0, 1), 768, 256, 0, "gg")
+        project((2,), 512, 512, 4, "gg")
+        project((3,), 512, 512, 5, "gg")

@@ -90,7 +90,10 @@ def tile_list_descriptor_power_compression_kernel(tc, tab_words, tab_scales, w1,
             nc.vector.tensor_copy(v_codes[a][:], tab[a][:].bitcast(U32).indirect(hits[:]))
 
         def prepare(g, a, cuts, by_slice):
-            grouped = ring.tile([P, PACK, P, PACK], BF16, name="grouped", align_bytes=64)
+            if by_slice:
+                grouped = keep.tile([P, PACK, P, PACK], BF16, name="slot_last", align_bytes=64)
+            else:
+                grouped = ring.tile([P, PACK, P, PACK], BF16, name="grouped", align_bytes=64, bufs=2)
             dst = grouped[:].rearrange("p (u e) m j -> p u m j e", e=2)
             codes = keep.tile([P, K_PASS], U32, name=f"w1_codes{g}{a}", align_bytes=64)
             scales = keep.tile([P, K_PASS], U8, name=f"w1_sc{g}{a}", align_bytes=64)
@@ -113,7 +116,7 @@ def tile_list_descriptor_power_compression_kernel(tc, tab_words, tab_scales, w1,
         nc.vector.tensor_copy(v_sc[:], tab_sc[:].bitcast(U8).indirect(hits[:]))
         for a in range(KP - 1):
             for g in range(HP):
-                prepare(g, a, (("s", 0, P, raw[a][:, :, g * K_PASS : (g + 1) * K_PASS]),), False)
+                prepare(g, a, (("v" if (g, a) == (1, 1) else "s", 0, P, raw[a][:, :, g * K_PASS : (g + 1) * K_PASS]),), False)
         half = S // 2
         gather(2)
         nc.vector.tensor_copy(v_codes[0][:], tab[0][:].bitcast(U32).indirect(hits[:, : half // 16]))
@@ -183,12 +186,17 @@ def tile_list_descriptor_power_compression_kernel(tc, tab_words, tab_scales, w1,
                             stop=(g == HP - 1),
                         )
             factor = weight[:, tok0 : tok0 + width].unsqueeze(1).to_broadcast(shape)
+            if how == "gg" and width * len(rows) == 256:
+                plain = ring.tile(shape, F32, name="plain")
+                nc.scalar.copy(plain[:], z[:])
+                weighted = ring.tile(shape, F32, name="weighted")
+                nc.gpsimd.tensor_tensor(weighted[:], plain[:], factor, MULT)
             if slot:
                 size = keep.tile(shape, F32, name=slot, align_bytes=64)
             else:
                 size = ring.tile(shape, F32, name="size")
             nc.scalar.activation(size[:], z[:], ACT.Abs)
-            if how == "gg":
+            if how == "gg" and width * len(rows) == 512:
                 plain = ring.tile(shape, F32, name="plain")
                 nc.scalar.copy(plain[:], z[:])
                 weighted = ring.tile(shape, F32, name="weighted")
@@ -202,7 +210,7 @@ def tile_list_descriptor_power_compression_kernel(tc, tab_words, tab_scales, w1,
                 if bare_slot:
                     bare = keep.tile(shape, F32, name=bare_slot, align_bytes=64)
                 else:
-                    bare = ring.tile(shape, F32, name="bare")
+                    bare = ring.tile(shape, F32, name="bare", bufs=2)
                 nc.vector.tensor_tensor(bare[:], z[:], inv[:], MULT)
                 y = bare
                 if how != "fused":
@@ -235,21 +243,20 @@ def tile_list_descriptor_power_compression_kernel(tc, tab_words, tab_scales, w1,
             sums(g, list(pair), acc, range(KP))
             hidden(g, pair, acc, False, slot)
 
+        hidden(0, (2, 3), accs[0], False, "slot_last")
         project((0,), 0, 256, 0, "fused", "slot_first0")
         project((1,), 0, 256, 1, "fused", "slot_first1")
-        for g in range(HP):
-            hidden(g, (2, 3), accs[g], False, f"slot_first{g}")
-        project((2,), 0, 256, 4, "fused")
-        project((3,), 0, 256, 5, "fused")
-        later(0, (4, 5), 2)
+        hidden(1, (2, 3), accs[1], False, "slot_first0")
+        project((2, 3), 0, 256, 4, "vv")
+        later(0, (4, 5), 2, "slot_first1")
         later(1, (4, 5), 6)
-        project((0,), 256, 256, 0, "fused")
-        project((1,), 256, 256, 1, "vg")
-        later(0, (6, 7), 2, "slot_late0")
-        later(1, (6, 7), 6, "slot_late1")
-        project((2,), 256, 256, 4, "vv", None, "slot_late0")
-        project((3,), 256, 256, 5, "vv", None, "slot_late1")
-        project((0, 1), 512, 256, 1, "gg")
-        project((0, 1), 768, 256, 0, "gg")
-        project((2,), 512, 512, 4, "gg")
-        project((3,), 512, 512, 5, "gg")
+        project((0,), 256, 256, 0, "gg")
+        project((1, 3), 256, 256, 1, "gg")
+        later(0, (6, 7), 2)
+        later(1, (6, 7), 6, "slot_late")
+        project((2,), 256, 256, 4, "fused", None, "slot_late")
+        project((0, 2), 512, 256, 5, "gg")
+        project((0,), 768, 256, 0, "gg")
+        project((2,), 768, 256, 1, "gg")
+        project((1,), 512, 512, 2, "gg")
+        project((3,), 512, 512, 3, "gg")

@@ -189,7 +189,10 @@ def tile_list_descriptor_power_compression_kernel(tc, tab_words, tab_scales, w1,
             if how == "gg" and width * len(rows) == 256:
                 plain = ring.tile(shape, F32, name="plain")
                 nc.scalar.copy(plain[:], z[:])
-                weighted = ring.tile(shape, F32, name="weighted")
+                if bare_slot:
+                    weighted = keep.tile(shape, F32, name=bare_slot, align_bytes=64)
+                else:
+                    weighted = ring.tile(shape, F32, name="weighted")
                 nc.gpsimd.tensor_tensor(weighted[:], plain[:], factor, MULT)
             if slot:
                 size = keep.tile(shape, F32, name=slot, align_bytes=64)
@@ -199,7 +202,10 @@ def tile_list_descriptor_power_compression_kernel(tc, tab_words, tab_scales, w1,
             if how == "gg" and width * len(rows) == 512:
                 plain = ring.tile(shape, F32, name="plain")
                 nc.scalar.copy(plain[:], z[:])
-                weighted = ring.tile(shape, F32, name="weighted")
+                if bare_slot:
+                    weighted = keep.tile(shape, F32, name=bare_slot, align_bytes=64)
+                else:
+                    weighted = ring.tile(shape, F32, name="weighted")
                 nc.gpsimd.tensor_tensor(weighted[:], plain[:], factor, MULT)
             inv = ring.tile(shape, F32, name="inv")
             nc.scalar.activation(inv[:], size[:], ACT.Abs_reciprocal_sqrt, bias=eps[:])
@@ -247,16 +253,15 @@ def tile_list_descriptor_power_compression_kernel(tc, tab_words, tab_scales, w1,
         project((0,), 0, 256, 0, "fused", "slot_first0")
         project((1,), 0, 256, 1, "fused", "slot_first1")
         hidden(1, (2, 3), accs[1], False, "slot_first0")
-        project((2, 3), 0, 256, 4, "vv")
+        project((2, 3), 0, 256, 4, "fused")
         later(0, (4, 5), 2, "slot_first1")
         later(1, (4, 5), 6)
-        project((0,), 256, 256, 0, "gg")
-        project((1, 3), 256, 256, 1, "gg")
-        later(0, (6, 7), 2)
-        later(1, (6, 7), 6, "slot_late")
-        project((2,), 256, 256, 4, "fused", None, "slot_late")
-        project((0, 2), 512, 256, 5, "gg")
-        project((0,), 768, 256, 0, "gg")
-        project((2,), 768, 256, 1, "gg")
-        project((1,), 512, 512, 2, "gg")
-        project((3,), 512, 512, 3, "gg")
+        project((0, 1), 256, 256, 5, "fused")
+        later(0, (6, 7), 2, "slot_late0")
+        later(1, (6, 7), 6, "slot_late1")
+        project((2,), 256, 256, 0, "vv", None, "slot_late0")
+        project((3,), 256, 256, 1, "vv", None, "slot_late1")
+        project((0, 1), 512, 256, 4, "gg", None, "slot_late1")
+        project((0, 1), 768, 256, 5, "gg", None, "slot_late1")
+        project((2,), 512, 512, 0, "gg")
+        project((3,), 512, 512, 1, "gg")

@@ -256,12 +256,12 @@ def tile_list_descriptor_power_compression_kernel(tc, tab_words, tab_scales, w1,
         project((2, 3), 0, 256, 4, "fused")
         later(0, (4, 5), 2, "slot_first1")
         later(1, (4, 5), 6)
-        project((0, 1), 256, 256, 5, "fused")
-        later(0, (6, 7), 2, "slot_late0")
-        later(1, (6, 7), 6, "slot_late1")
-        project((2,), 256, 256, 0, "vv", None, "slot_late0")
-        project((3,), 256, 256, 1, "vv", None, "slot_late1")
-        project((0, 1), 512, 256, 4, "gg", None, "slot_late1")
-        project((0, 1), 768, 256, 5, "gg", None, "slot_late1")
-        project((2,), 512, 512, 0, "gg")
-        project((3,), 512, 512, 1, "gg")
+        later(0, (6, 7), 0, "slot_late0")
+        later(1, (6, 7), 2, "slot_late1")
+        project((0,), 256, 256, 5, "vv", None, "slot_late0")
+        project((1,), 256, 256, 4, "vv", None, "slot_late1")
+        project((2, 3), 256, 256, 6, "gg", None, "slot_late1")
+        project((0, 1), 512, 256, 7, "gg", None, "slot_late1")
+        project((0, 1), 768, 256, 0, "gg", None, "slot_late1")
+        project((2,), 512, 512, 1, "gg")
+        project((3,), 512, 512, 2, "gg")

@@ -30,6 +30,7 @@ def tile_list_descriptor_power_compression_kernel(tc, tab_words, tab_scales, w1,
     with ExitStack() as ctx:
         keep = ctx.enter_context(tc.tile_pool(name="keep", bufs=1))
         ring = ctx.enter_context(tc.tile_pool(name="ring", bufs=3))
+        reuse = ctx.enter_context(tc.tile_pool(name="reuse", bufs=1))
         psum = ctx.enter_context(tc.psum_pool(name="psum", bufs=1))
 
         hits = keep.tile([P, S // 16], U16, name="hits")
@@ -40,47 +41,47 @@ def tile_list_descriptor_power_compression_kernel(tc, tab_words, tab_scales, w1,
         nc.gpsimd.memset(hundred[:], 100.0)
         nc.scalar.activation(eps[:], hundred[:], ACT.Abs_reciprocal_sqrt)
 
-        tab_sc = keep.tile([P, T // 4], I32, name="tab_sc", align_bytes=64)
-        nc.vector.memset(tab_sc[:], 0)
-        w2_sc = keep.tile([P, HP * N // 4], I32, name="w2_sc", align_bytes=64)
+        tab_sc = [reuse.tile([P, T // 4], I32, name=f"tab_sc{a}", align_bytes=64, offset=(0, T, 4 * T - T // 2)[a]) for a in range(KP)]
+        for a in range(KP):
+            nc.vector.memset(tab_sc[a][:], 0)
+        planes = keep.tile([P, KP * S // 4], I32, name="planes", align_bytes=64)
+        nc.vector.memset(planes[:], 0)
 
-        tab = [keep.tile([P, T], I32, name=f"tab{a}", align_bytes=64) for a in range(KP)]
+        tab = {0: reuse.tile([P, T], I32, name="tab0", align_bytes=64, offset=8 * T), 2: keep.tile([P, T], I32, name="tab2", align_bytes=64)}
         words = [tab_words[a].rearrange("p t i -> p (t i)").bitcast(I32) for a in range(KP)]
         raw = [keep.tile([P, PACK, H], F32, name=f"raw{a}") for a in range(KP - 1)]
         rows = [w1[a * K_PASS : (a + 1) * K_PASS, :].rearrange("(p j) c -> p j c", j=PACK) for a in range(KP)]
-        for j in range(PACK):
-            nc.sync.dma_start(raw[0][:, j, :], rows[0][:, j, :])
+        nc.sync.dma_start(raw[0][:, 0, :], rows[0][:, 0, :])
         nc.sync.dma_start(hits[:], offs)
+        nc.sync.dma_start(raw[0][:, 1, :], rows[0][:, 1, :])
+        for g in range(HP):
+            for j in (2, 3):
+                nc.sync.dma_start(raw[0][:, j, g * K_PASS : (g + 1) * K_PASS], rows[0][:, j, g * K_PASS : (g + 1) * K_PASS])
         nc.sync.dma_start(places[:], offs2)
-        for q in range(4):
-            nc.sync.dma_start(tab_sc[32 * q : 32 * q + 4 * KP, :], tab_scales[:, 4 * q : 4 * q + 4, :].bitcast(I32))
-        nc.vector.memset(w2_sc[:], 0)
+        for a in range(KP):
+            nc.sync.dma_start(tab_sc[a][0:P:8, :], tab_scales[a].bitcast(I32))
         nc.sync.dma_start(tab[2][:], words[2])
         nc.sync.dma_start(raw[1][:], rows[1])
         nc.sync.dma_start(tab[0][:], words[0])
-        nc.sync.dma_start(tab[1][:], words[1])
-        last = {}
-        for c0, c1 in ((0, 512), (512, 768), (768, 1024)):
-            last[c0] = keep.tile([P, PACK, c1 - c0], F32, name=f"last{c0}")
-            nc.sync.dma_start(last[c0][:], rows[2][:, :, c0:c1])
-
-        for q in range(4):
-            nc.sync.dma_start(
-                w2_sc[32 * q : 32 * q + 4, :].rearrange("r (a c) -> r a c", a=HP),
-                w2_scales[:, 4 * q : 4 * q + 4, :].rearrange("a r c -> r a c").bitcast(I32),
-            )
-        w2_codes = keep.tile([P, HP, 2 * N // 4], I32, name="w2_codes", align_bytes=64)
-        nc.sync.dma_start(w2_codes[:], w2_words.rearrange("a p c -> p a c").bitcast(I32))
-        weight = keep.tile([P, S], F32, name="weight")
-        nc.sync.dma_start(weight[:], wgo)
-
         cache = []
         for n in range(NT):
             window = keep.tile([P, T2], F32, name=f"cache{n}")
             nc.vector.memset(window[:], 0.0)
             cache.append(window)
 
-        v_sc = keep.tile([P, S], U8, name="v_sc", align_bytes=64)
+        picked_sc = reuse.tile([P, KP * S], U8, name="picked_sc", align_bytes=64, offset=7 * T - S)
+        for a in range(KP):
+            nc.vector.tensor_copy(picked_sc[:, a * S : (a + 1) * S], tab_sc[a][:].bitcast(U8).indirect(hits[:]))
+        for q in range(4):
+            nc.sync.dma_start(planes[32 * q : 32 * q + 4, :], picked_sc[32 * q : 32 * q + 32 : 8, :].bitcast(I32))
+        tab[1] = reuse.tile([P, T], I32, name="tab1", align_bytes=64, offset=0)
+        nc.sync.dma_start(tab[1][:], words[1])
+        last = {}
+        for c0, c1 in ((0, 512), (512, 768), (768, 1024)):
+            last[c0] = reuse.tile([P, PACK, c1 - c0], F32, name=f"last{c0}", offset=4 * T + 16 * c0)
+            nc.sync.dma_start(last[c0][:], rows[2][:, :, c0:c1])
+
+        v_sc = planes[:].bitcast(U8)
         v_codes = [keep.tile([P, S if a == 2 else S // 2], U32, name=f"v_codes{a}", align_bytes=64) for a in range(KP)]
         v_late = [keep.tile([P, S // 2], U32, name="v_late0", align_bytes=64)]
         w1_codes = {}
@@ -113,7 +114,6 @@ def tile_list_descriptor_power_compression_kernel(tc, tab_words, tab_scales, w1,
             w1_codes[g, a] = codes
             w1_sc[g, a] = scales
 
-        nc.vector.tensor_copy(v_sc[:], tab_sc[:].bitcast(U8).indirect(hits[:]))
         for a in range(KP - 1):
             for g in range(HP):
                 prepare(g, a, (("v" if (g, a) == (1, 1) else "s", 0, P, raw[a][:, :, g * K_PASS : (g + 1) * K_PASS]),), False)
@@ -121,6 +121,18 @@ def tile_list_descriptor_power_compression_kernel(tc, tab_words, tab_scales, w1,
         gather(2)
         nc.vector.tensor_copy(v_codes[0][:], tab[0][:].bitcast(U32).indirect(hits[:, : half // 16]))
         nc.vector.tensor_copy(v_late[0][:], tab[0][:].bitcast(U32).indirect(hits[:, half // 16 :]))
+        w2_sc = reuse.tile([P, HP * N // 4], I32, name="w2_sc", align_bytes=64, offset=8 * T)
+        nc.vector.memset(w2_sc[:], 0)
+        for q in range(4):
+            nc.sync.dma_start(
+                w2_sc[32 * q : 32 * q + 4, :].rearrange("r (a c) -> r a c", a=HP),
+                w2_scales[:, 4 * q : 4 * q + 4, :].rearrange("a r c -> r a c").bitcast(I32),
+            )
+        w2_codes = reuse.tile([P, HP, 2 * N // 4], I32, name="w2_codes", align_bytes=64, offset=9 * T)
+        nc.sync.dma_start(w2_codes[:], w2_words.rearrange("a p c -> p a c").bitcast(I32))
+        weight = reuse.tile([P, S], F32, name="weight", offset=10 * T)
+        nc.sync.dma_start(weight[:], wgo)
+
         nc.vector.tensor_copy(v_codes[1][:], tab[1][:].bitcast(U32).indirect(hits[:, : half // 16]))
         prepare(0, KP - 1, (("v", 0, 80, last[0][:, :, 0:320]), ("s", 80, P, last[0][:, :, 320:512])), False)
         prepare(1, KP - 1, (("s", 0, 64, last[512][:]), ("v", 64, P, last[768][:])), True)
@@ -140,7 +152,7 @@ def tile_list_descriptor_power_compression_kernel(tc, tab_words, tab_scales, w1,
                                 lhsT=w1_codes[g, a][:, t * P : (t + 1) * P].bitcast(FP8X4),
                                 lhsT_scale=w1_sc[g, a][:, t * P : (t + 1) * P],
                                 rhs=(v_late[a][:, b * BLK - half : (b + 1) * BLK - half] if a < 2 and b >= 4 else v_codes[a][:, cols]).bitcast(FP8X4),
-                                rhs_scale=v_sc[4 * a : P, cols],
+                                rhs_scale=v_sc[:, a * S + b * BLK : a * S + (b + 1) * BLK],
                                 start=(a == 0 and t == 0),
                                 stop=(a == KP - 1 and t == PACK - 1),
                             )

@@ -43,7 +43,7 @@ def tile_list_descriptor_power_compression_kernel(tc, tab_words, tab_scales, w1,
 
         tab_sc = [reuse.tile([P, T // 4], I32, name=f"tab_sc{a}", align_bytes=64, offset=(0, T, 4 * T - T // 2)[a]) for a in range(KP)]
         for a in range(KP):
-            nc.vector.memset(tab_sc[a][:], 0)
+            (nc.gpsimd if a == 1 else nc.vector).memset(tab_sc[a][:], 0)
         planes = keep.tile([P, KP * S // 4], I32, name="planes", align_bytes=64)
         nc.vector.memset(planes[:], 0)
 
@@ -51,13 +51,14 @@ def tile_list_descriptor_power_compression_kernel(tc, tab_words, tab_scales, w1,
         words = [tab_words[a].rearrange("p t i -> p (t i)").bitcast(I32) for a in range(KP)]
         raw = [keep.tile([P, PACK, H], F32, name=f"raw{a}") for a in range(KP - 1)]
         rows = [w1[a * K_PASS : (a + 1) * K_PASS, :].rearrange("(p j) c -> p j c", j=PACK) for a in range(KP)]
-        nc.sync.dma_start(raw[0][:, 0, :], rows[0][:, 0, :])
+        nc.sync.dma_start(raw[0][:, 2, :K_PASS], rows[0][:, 2, :K_PASS])
         nc.sync.dma_start(hits[:], offs)
-        nc.sync.dma_start(raw[0][:, 1, :], rows[0][:, 1, :])
-        for g in range(HP):
-            for j in (2, 3):
-                nc.sync.dma_start(raw[0][:, j, g * K_PASS : (g + 1) * K_PASS], rows[0][:, j, g * K_PASS : (g + 1) * K_PASS])
+        nc.sync.dma_start(raw[0][:, 3, :K_PASS], rows[0][:, 3, :K_PASS])
         nc.sync.dma_start(places[:], offs2)
+        for j in (0, 1):
+            nc.sync.dma_start(raw[0][:, j, :], rows[0][:, j, :])
+        for j in (2, 3):
+            nc.sync.dma_start(raw[0][:, j, K_PASS:], rows[0][:, j, K_PASS:])
         for a in range(KP):
             nc.sync.dma_start(tab_sc[a][0:P:8, :], tab_scales[a].bitcast(I32))
         nc.sync.dma_start(tab[2][:], words[2])

@@ -135,6 +135,8 @@ def tile_list_descriptor_power_compression_kernel(tc, tab_words, tab_scales, w1,
         nc.sync.dma_start(weight[:], wgo)
 
         nc.vector.tensor_copy(v_codes[1][:], tab[1][:].bitcast(U32).indirect(hits[:, : half // 16]))
+        v_late.append(keep.tile([P, half], U32, name="v_late1", align_bytes=64))
+        nc.vector.tensor_copy(v_late[1][:], tab[1][:].bitcast(U32).indirect(hits[:, half // 16 :]))
         prepare(0, KP - 1, (("v", 0, 80, last[0][:, :, 0:320]), ("s", 80, P, last[0][:, :, 320:512])), False)
         prepare(1, KP - 1, (("s", 0, 64, last[512][:]), ("v", 64, P, last[768][:])), True)
 
@@ -158,14 +160,14 @@ def tile_list_descriptor_power_compression_kernel(tc, tab_words, tab_scales, w1,
                                 stop=(a == KP - 1 and t == PACK - 1),
                             )
 
-        def hidden(g, pair, accs, first, slot=None):
+        def hidden(g, pair, accs, first, slot=None, onv=False):
             if slot:
                 relu = keep.tile([P, 2 * BLK, PACK], BF16, name=slot, align_bytes=64)
             else:
                 relu = ring.tile([P, 2 * BLK, PACK], BF16, name="relu", align_bytes=64)
             for i, b in enumerate(pair):
                 part = relu[:, i * BLK : (i + 1) * BLK, :]
-                if first and i == 1:
+                if onv or (first and i == 1):
                     nc.vector.tensor_scalar_max(part, accs[b][:].rearrange("p t n -> p n t"), 0.0)
                 else:
                     nc.scalar.activation(part, accs[b][:].rearrange("p t n -> p n t"), ACT.Relu)
@@ -253,8 +255,6 @@ def tile_list_descriptor_power_compression_kernel(tc, tab_words, tab_scales, w1,
         sums(0, [2, 3], accs[0], (KP - 1,))
         sums(1, [0, 1], accs[1], (KP - 1,))
         hidden(1, (0, 1), accs[1], True, "slot_gather")
-        v_late.append(keep.tile([P, half], U32, name="slot_gather", align_bytes=64))
-        nc.vector.tensor_copy(v_late[1][:], tab[1][:].bitcast(U32).indirect(hits[:, half // 16 :]))
         sums(1, [2, 3], accs[1], (KP - 1,))
 
         def later(g, pair, first_bank, slot=None):
@@ -262,19 +262,20 @@ def tile_list_descriptor_power_compression_kernel(tc, tab_words, tab_scales, w1,
             sums(g, list(pair), acc, range(KP))
             hidden(g, pair, acc, False, slot)
 
+        hidden(1, (2, 3), accs[1], False, "slot_gather", True)
         hidden(0, (2, 3), accs[0], False, "slot_last")
         project((0,), 0, 256, 0, "fused", "slot_first0")
         project((1,), 0, 256, 1, "fused", "slot_first1")
-        hidden(1, (2, 3), accs[1], False, "slot_first0")
-        project((2, 3), 0, 256, 4, "fused")
-        later(0, (4, 5), 2, "slot_first1")
-        later(1, (4, 5), 6)
+        later(0, (4, 5), 2, "slot_first0")
+        project((2,), 0, 256, 4, "fused")
+        later(1, (4, 5), 6, "slot_first1")
         later(0, (6, 7), 0, "slot_late0")
         later(1, (6, 7), 2, "slot_late1")
-        project((0,), 256, 256, 5, "vv", None, "slot_late0")
-        project((1,), 256, 256, 4, "vv", None, "slot_late1")
-        project((2, 3), 256, 256, 6, "gg", None, "slot_late1")
-        project((0, 1), 512, 256, 7, "gg", None, "slot_late1")
-        project((0, 1), 768, 256, 0, "gg", None, "slot_late1")
-        project((2,), 512, 512, 1, "gg")
-        project((3,), 512, 512, 2, "gg")
+        project((3,), 0, 256, 5, "vv", None, "slot_late0")
+        project((0,), 256, 256, 6, "vv", None, "slot_late1")
+        project((1, 2), 256, 256, 7, "gg", None, "slot_late1")
+        project((3,), 256, 512, 4, "gg", None, "slot_late1")
+        project((0, 1), 512, 256, 0, "gg", None, "slot_late1")
+        project((0, 1), 768, 256, 1, "gg", None, "slot_late1")
+        project((3,), 768, 256, 2, "gg", None, "slot_late1")
+        project((2,), 512, 512, 3, "gg", None, "slot_late1")

@@ -32,6 +32,8 @@ def tile_list_descriptor_power_compression_kernel(tc, tab_words, tab_scales, w1,
         ring = ctx.enter_context(tc.tile_pool(name="ring", bufs=3))
         reuse = ctx.enter_context(tc.tile_pool(name="reuse", bufs=1))
         psum = ctx.enter_context(tc.psum_pool(name="psum", bufs=1))
+        KB = 1024
+        half = S // 2
 
         hits = keep.tile([P, S // 16], U16, name="hits")
         places = keep.tile([P, S // 16], U16, name="places")
@@ -41,61 +43,52 @@ def tile_list_descriptor_power_compression_kernel(tc, tab_words, tab_scales, w1,
         nc.gpsimd.memset(hundred[:], 100.0)
         nc.scalar.activation(eps[:], hundred[:], ACT.Abs_reciprocal_sqrt)
 
-        tab_sc = [reuse.tile([P, T // 4], I32, name=f"tab_sc{a}", align_bytes=64, offset=(0, T, 4 * T - T // 2)[a]) for a in range(KP)]
-        for a in range(KP):
-            (nc.gpsimd if a == 1 else nc.vector).memset(tab_sc[a][:], 0)
+        tab_sc = reuse.tile([P, KP, T // 4], I32, name="tab_sc", align_bytes=64, offset=8 * KB)
+        nc.vector.memset(tab_sc[:], 0)
         planes = keep.tile([P, KP * S // 4], I32, name="planes", align_bytes=64)
         nc.vector.memset(planes[:], 0)
-
-        tab = {0: reuse.tile([P, T], I32, name="tab0", align_bytes=64, offset=8 * T), 2: keep.tile([P, T], I32, name="tab2", align_bytes=64)}
-        words = [tab_words[a].rearrange("p t i -> p (t i)").bitcast(I32) for a in range(KP)]
-        raw = [keep.tile([P, PACK, H], F32, name=f"raw{a}") for a in range(KP - 1)]
-        rows = [w1[a * K_PASS : (a + 1) * K_PASS, :].rearrange("(p j) c -> p j c", j=PACK) for a in range(KP)]
-        nc.sync.dma_start(raw[0][:, 2, :K_PASS], rows[0][:, 2, :K_PASS])
-        nc.sync.dma_start(hits[:], offs)
-        nc.sync.dma_start(raw[0][:, 3, :K_PASS], rows[0][:, 3, :K_PASS])
-        nc.sync.dma_start(places[:], offs2)
-        for j in (0, 1):
-            nc.sync.dma_start(raw[0][:, j, :], rows[0][:, j, :])
-        for j in (2, 3):
-            nc.sync.dma_start(raw[0][:, j, K_PASS:], rows[0][:, j, K_PASS:])
-        for a in range(KP):
-            nc.sync.dma_start(tab_sc[a][0:P:8, :], tab_scales[a].bitcast(I32))
-        nc.sync.dma_start(tab[2][:], words[2])
-        nc.sync.dma_start(raw[1][:], rows[1])
-        nc.sync.dma_start(tab[0][:], words[0])
         cache = []
         for n in range(NT):
             window = keep.tile([P, T2], F32, name=f"cache{n}")
             nc.vector.memset(window[:], 0.0)
             cache.append(window)
 
-        picked_sc = reuse.tile([P, KP * S], U8, name="picked_sc", align_bytes=64, offset=7 * T - S)
+        tab = {0: keep.tile([P, T], I32, name="tab0", align_bytes=64), 1: reuse.tile([P, T], I32, name="tab1", align_bytes=64, offset=32 * KB)}
+        words = [tab_words[a].rearrange("p t i -> p (t i)").bitcast(I32) for a in range(KP)]
+        raw = [keep.tile([P, PACK, H], F32, name=f"raw{a}") for a in range(KP - 1)]
+        rows = [w1[a * K_PASS : (a + 1) * K_PASS, :].rearrange("(p j) c -> p j c", j=PACK) for a in range(KP)]
+        nc.sync.dma_start(raw[0][:], rows[0])
+        nc.sync.dma_start(hits[:], offs)
+        nc.sync.dma_start(tab_sc[0:P:8, :, :], tab_scales.rearrange("a r c -> r a c").bitcast(I32))
+        nc.sync.dma_start(places[:], offs2)
+        nc.sync.dma_start(tab[0][:], words[0])
+        nc.sync.dma_start(raw[1][:], rows[1])
+        nc.sync.dma_start(tab[1][:], words[1])
+
+        picked_sc = reuse.tile([P, KP * S], U8, name="picked_sc", align_bytes=64, offset=48 * KB)
         for a in range(KP):
-            nc.vector.tensor_copy(picked_sc[:, a * S : (a + 1) * S], tab_sc[a][:].bitcast(U8).indirect(hits[:]))
+            nc.vector.tensor_copy(picked_sc[:, a * S : (a + 1) * S], tab_sc[:, a, :].bitcast(U8).indirect(hits[:]))
+        tab[2] = reuse.tile([P, T], I32, name="tab2", align_bytes=64, offset=0)
+        nc.sync.dma_start(tab[2][:, : T // 2], words[2][:, : T // 2])
         for q in range(4):
             nc.sync.dma_start(planes[32 * q : 32 * q + 4, :], picked_sc[32 * q : 32 * q + 32 : 8, :].bitcast(I32))
-        tab[1] = reuse.tile([P, T], I32, name="tab1", align_bytes=64, offset=0)
-        nc.sync.dma_start(tab[1][:], words[1])
+        nc.sync.dma_start(tab[2][:, T // 2 :], words[2][:, T // 2 :])
         last = {}
         for c0, c1 in ((0, 512), (512, 768), (768, 1024)):
-            last[c0] = reuse.tile([P, PACK, c1 - c0], F32, name=f"last{c0}", offset=4 * T + 16 * c0)
+            last[c0] = reuse.tile([P, PACK, c1 - c0], F32, name=f"last{c0}", offset=16 * KB + 16 * c0)
             nc.sync.dma_start(last[c0][:], rows[2][:, :, c0:c1])
 
         v_sc = planes[:].bitcast(U8)
-        v_codes = [keep.tile([P, S if a == 2 else S // 2], U32, name=f"v_codes{a}", align_bytes=64) for a in range(KP)]
-        v_late = [keep.tile([P, S // 2], U32, name="v_late0", align_bytes=64)]
+        v_codes = {}
         w1_codes = {}
         w1_sc = {}
 
-        def gather(a):
-            nc.vector.tensor_copy(v_codes[a][:], tab[a][:].bitcast(U32).indirect(hits[:]))
+        def gather(a, s):
+            v_codes[a, s] = keep.tile([P, half], U32, name=f"v_codes{a}{s}", align_bytes=64)
+            nc.vector.tensor_copy(v_codes[a, s][:], tab[a][:].bitcast(U32).indirect(hits[:, s * half // 16 : (s + 1) * half // 16]))
 
         def prepare(g, a, cuts, by_slice):
-            if by_slice:
-                grouped = keep.tile([P, PACK, P, PACK], BF16, name="slot_last", align_bytes=64)
-            else:
-                grouped = ring.tile([P, PACK, P, PACK], BF16, name="grouped", align_bytes=64, bufs=2)
+            grouped = ring.tile([P, PACK, P, PACK], BF16, name="grouped", align_bytes=64, bufs=2)
             dst = grouped[:].rearrange("p (u e) m j -> p u m j e", e=2)
             codes = keep.tile([P, K_PASS], U32, name=f"w1_codes{g}{a}", align_bytes=64)
             scales = keep.tile([P, K_PASS], U8, name=f"w1_sc{g}{a}", align_bytes=64)
@@ -118,74 +111,64 @@ def tile_list_descriptor_power_compression_kernel(tc, tab_words, tab_scales, w1,
         for a in range(KP - 1):
             for g in range(HP):
                 prepare(g, a, (("v" if (g, a) == (1, 1) else "s", 0, P, raw[a][:, :, g * K_PASS : (g + 1) * K_PASS]),), False)
-        half = S // 2
-        gather(2)
-        nc.vector.tensor_copy(v_codes[0][:], tab[0][:].bitcast(U32).indirect(hits[:, : half // 16]))
-        nc.vector.tensor_copy(v_late[0][:], tab[0][:].bitcast(U32).indirect(hits[:, half // 16 :]))
-        w2_sc = reuse.tile([P, HP * N // 4], I32, name="w2_sc", align_bytes=64, offset=8 * T)
+        for a in (0, 1):
+            for s in range(2):
+                gather(a, s)
+        w2_sc = reuse.tile([P, HP * N // 4], I32, name="w2_sc", align_bytes=64, offset=32 * KB)
         nc.vector.memset(w2_sc[:], 0)
         for q in range(4):
             nc.sync.dma_start(
                 w2_sc[32 * q : 32 * q + 4, :].rearrange("r (a c) -> r a c", a=HP),
                 w2_scales[:, 4 * q : 4 * q + 4, :].rearrange("a r c -> r a c").bitcast(I32),
             )
-        w2_codes = reuse.tile([P, HP, 2 * N // 4], I32, name="w2_codes", align_bytes=64, offset=9 * T)
+        w2_codes = reuse.tile([P, HP, 2 * N // 4], I32, name="w2_codes", align_bytes=64, offset=36 * KB)
         nc.sync.dma_start(w2_codes[:], w2_words.rearrange("a p c -> p a c").bitcast(I32))
-        weight = reuse.tile([P, S], F32, name="weight", offset=10 * T)
+        weight = reuse.tile([P, S], F32, name="weight", offset=40 * KB)
         nc.sync.dma_start(weight[:], wgo)
 
-        nc.vector.tensor_copy(v_codes[1][:], tab[1][:].bitcast(U32).indirect(hits[:, : half // 16]))
-        v_late.append(keep.tile([P, half], U32, name="v_late1", align_bytes=64))
-        nc.vector.tensor_copy(v_late[1][:], tab[1][:].bitcast(U32).indirect(hits[:, half // 16 :]))
-        prepare(0, KP - 1, (("v", 0, 80, last[0][:, :, 0:320]), ("s", 80, P, last[0][:, :, 320:512])), False)
+        for s in range(2):
+            gather(2, s)
+        prepare(0, KP - 1, (("v", 0, 80, last[0][:, :, 0:320]), ("s", 80, P, last[0][:, :, 320:512])), True)
         prepare(1, KP - 1, (("s", 0, 64, last[512][:]), ("v", 64, P, last[768][:])), True)
 
         h_codes = [keep.tile([P, S], U32, name=f"h_codes{g}", align_bytes=64) for g in range(HP)]
         h_sc = [keep.tile([P, S], U8, name=f"h_sc{g}", align_bytes=64) for g in range(HP)]
         w2_sc_bytes = w2_sc[:].bitcast(U8)
 
-        def sums(g, blocks, accs, passes):
+        def sums(g, pair, accs, passes):
             for a in passes:
-                for b0 in range(0, len(blocks), 2):
-                    for t in range(PACK):
-                        for b in blocks[b0 : b0 + 2]:
-                            cols = slice(b * BLK, (b + 1) * BLK)
-                            nc.tensor.matmul_mx(
-                                out=accs[b][:, t, :],
-                                lhsT=w1_codes[g, a][:, t * P : (t + 1) * P].bitcast(FP8X4),
-                                lhsT_scale=w1_sc[g, a][:, t * P : (t + 1) * P],
-                                rhs=(v_late[a][:, b * BLK - half : (b + 1) * BLK - half] if a < 2 and b >= 4 else v_codes[a][:, cols]).bitcast(FP8X4),
-                                rhs_scale=v_sc[:, a * S + b * BLK : a * S + (b + 1) * BLK],
-                                start=(a == 0 and t == 0),
-                                stop=(a == KP - 1 and t == PACK - 1),
-                            )
+                for t in range(PACK):
+                    for b in pair:
+                        s, c0 = divmod(b * BLK, half)
+                        nc.tensor.matmul_mx(
+                            out=accs[b][:, t, :],
+                            lhsT=w1_codes[g, a][:, t * P : (t + 1) * P].bitcast(FP8X4),
+                            lhsT_scale=w1_sc[g, a][:, t * P : (t + 1) * P],
+                            rhs=v_codes[a, s][:, c0 : c0 + BLK].bitcast(FP8X4),
+                            rhs_scale=v_sc[:, a * S + b * BLK : a * S + (b + 1) * BLK],
+                            start=(a == 0 and t == 0),
+                            stop=(a == KP - 1 and t == PACK - 1),
+                        )
 
-        def hidden(g, pair, accs, first, slot=None, onv=False):
-            if slot:
-                relu = keep.tile([P, 2 * BLK, PACK], BF16, name=slot, align_bytes=64)
-            else:
-                relu = ring.tile([P, 2 * BLK, PACK], BF16, name="relu", align_bytes=64)
+        def quantise_h(g, b0, blocks, relu):
+            cols = slice(b0 * BLK, (b0 + blocks) * BLK)
+            nc.vector.quantize_mx(out=h_codes[g][:, cols].bitcast(FP8X4), scales=h_sc[g][:, cols], in_=relu.rearrange("p n t -> p (n t)"))
+
+        def empty(g, pair, accs, slot, on_vector=(False, False)):
+            relu = keep.tile([P, len(pair) * BLK, PACK], BF16, name=slot, align_bytes=64)
             for i, b in enumerate(pair):
                 part = relu[:, i * BLK : (i + 1) * BLK, :]
-                if onv or (first and i == 1):
+                if on_vector[i]:
                     nc.vector.tensor_scalar_max(part, accs[b][:].rearrange("p t n -> p n t"), 0.0)
                 else:
                     nc.scalar.activation(part, accs[b][:].rearrange("p t n -> p n t"), ACT.Relu)
-            if first:
-                for i, b in enumerate(pair):
-                    cols = slice(b * BLK, (b + 1) * BLK)
-                    part = relu[:, i * BLK : (i + 1) * BLK, :]
-                    nc.vector.quantize_mx(out=h_codes[g][:, cols].bitcast(FP8X4), scales=h_sc[g][:, cols], in_=part.rearrange("p n t -> p (n t)"))
-            else:
-                cols = slice(pair[0] * BLK, (pair[1] + 1) * BLK)
-                nc.vector.quantize_mx(out=h_codes[g][:, cols].bitcast(FP8X4), scales=h_sc[g][:, cols], in_=relu[:].rearrange("p n t -> p (n t)"))
+            return relu
 
-        def banks(blocks, first_bank):
-            return {b: psum.tile([P, PACK, BLK], F32, name=f"bank{first_bank + i}") for i, b in enumerate(blocks)}
+        def banks(blocks, numbers):
+            return {b: psum.tile([P, PACK, BLK], F32, name=f"bank{i}") for b, i in zip(blocks, numbers)}
 
-        def project(rows, tok0, width, bank, how, slot=None, bare_slot=None):
-            shape = [P, len(rows), width]
-            z = psum.tile(shape, F32, name=f"bank{bank}")
+        def product(rows, tok0, width, bank):
+            z = psum.tile([P, len(rows), width], F32, name=f"bank{bank}")
             step = width if width == 512 else BLK
             for i, n in enumerate(rows):
                 for c0 in range(0, width, step):
@@ -200,82 +183,80 @@ def tile_list_descriptor_power_compression_kernel(tc, tab_words, tab_scales, w1,
                             start=(g == 0),
                             stop=(g == HP - 1),
                         )
-            factor = weight[:, tok0 : tok0 + width].unsqueeze(1).to_broadcast(shape)
-            if how == "gg" and width * len(rows) == 256:
-                plain = ring.tile(shape, F32, name="plain")
-                nc.scalar.copy(plain[:], z[:])
-                if bare_slot:
-                    weighted = keep.tile(shape, F32, name=bare_slot, align_bytes=64)
-                else:
-                    weighted = ring.tile(shape, F32, name="weighted")
-                nc.gpsimd.tensor_tensor(weighted[:], plain[:], factor, MULT)
-            if slot:
-                size = keep.tile(shape, F32, name=slot, align_bytes=64)
-            else:
-                size = ring.tile(shape, F32, name="size")
+            return z
+
+        def begin(rows, tok0, width, bank, slot, plain_slot="plain"):
+            shape = [P, len(rows), width]
+            z = product(rows, tok0, width, bank)
+            plain = keep.tile(shape, F32, name=plain_slot)
+            nc.scalar.copy(plain[:], z[:])
+            size = ring.tile(shape, F32, name="size", bufs=1)
             nc.scalar.activation(size[:], z[:], ACT.Abs)
-            if how == "gg" and width * len(rows) == 512:
-                plain = ring.tile(shape, F32, name="plain")
-                nc.scalar.copy(plain[:], z[:])
-                if bare_slot:
-                    weighted = keep.tile(shape, F32, name=bare_slot, align_bytes=64)
-                else:
-                    weighted = ring.tile(shape, F32, name="weighted")
-                nc.gpsimd.tensor_tensor(weighted[:], plain[:], factor, MULT)
-            inv = ring.tile(shape, F32, name="inv")
-            nc.scalar.activation(inv[:], size[:], ACT.Abs_reciprocal_sqrt, bias=eps[:])
-            if how == "gg":
-                y = ring.tile(shape, F32, name="y")
-                nc.gpsimd.tensor_tensor(y[:], weighted[:], inv[:], MULT)
+            weighted = keep.tile(shape, F32, name=slot, align_bytes=64)
+            nc.gpsimd.tensor_tensor(weighted[:], plain[:], weight[:, tok0 : tok0 + width].unsqueeze(1).to_broadcast(shape), MULT)
+            return rows, tok0, width, size, weighted
+
+        def finish(rows, tok0, width, size, weighted, inv_slot=None):
+            shape = [P, len(rows), width]
+            if inv_slot:
+                inv = keep.tile(shape, F32, name=inv_slot, align_bytes=64)
             else:
-                if bare_slot:
-                    bare = keep.tile(shape, F32, name=bare_slot, align_bytes=64)
-                else:
-                    bare = ring.tile(shape, F32, name="bare", bufs=2)
-                nc.vector.tensor_tensor(bare[:], z[:], inv[:], MULT)
-                y = bare
-                if how != "fused":
-                    y = ring.tile(shape, F32, name="y")
-                    (nc.vector if how == "vv" else nc.gpsimd).tensor_tensor(y[:], bare[:], factor, MULT)
+                inv = ring.tile(shape, F32, name="inv", bufs=2)
+            nc.scalar.activation(inv[:], size[:], ACT.Abs_reciprocal_sqrt, bias=eps[:])
+            y = ring.tile(shape, F32, name="y")
+            nc.gpsimd.tensor_tensor(y[:], weighted[:], inv[:], MULT)
             for i, n in enumerate(rows):
-                where = places[:, tok0 // 16 : (tok0 + width) // 16]
-                if how == "fused":
-                    nc.vector.tensor_tensor(cache[n][:].indirect(where), y[:, i, :], weight[:, tok0 : tok0 + width], MULT)
-                else:
-                    nc.vector.tensor_copy(cache[n][:].indirect(where), y[:, i, :])
+                nc.vector.tensor_copy(cache[n][:].indirect(places[:, tok0 // 16 : (tok0 + width) // 16]), y[:, i, :])
                 if tok0 + width == S:
                     nc.sync.dma_start(out[n * P : (n + 1) * P, :], cache[n][:])
 
-        accs = [banks((0, 1, 2, 3), 4 * g) for g in range(HP)]
+        accs = [banks((0, 1, 2, 3), range(4 * g, 4 * g + 4)) for g in range(HP)]
         for a in range(KP - 1):
             for g in range(HP):
-                sums(g, [0, 1, 2, 3], accs[g], (a,))
-        sums(0, [0, 1], accs[0], (KP - 1,))
-        hidden(0, (0, 1), accs[0], False)
-        sums(0, [2, 3], accs[0], (KP - 1,))
-        sums(1, [0, 1], accs[1], (KP - 1,))
-        hidden(1, (0, 1), accs[1], True, "slot_gather")
-        sums(1, [2, 3], accs[1], (KP - 1,))
+                for pair in ((0, 1), (2, 3)):
+                    sums(g, pair, accs[g], (a,))
+        sums(0, (0, 1), accs[0], (KP - 1,))
+        quantise_h(0, 0, 2, empty(0, (0, 1), accs[0], "relu_a")[:])
+        sums(0, (2, 3), accs[0], (KP - 1,))
+        sums(1, (0, 1), accs[1], (KP - 1,))
+        relu = empty(1, (0, 1), accs[1], "relu_b", (False, True))
+        for b in range(2):
+            quantise_h(1, b, 1, relu[:, b * BLK : (b + 1) * BLK, :])
+        sums(1, (2, 3), accs[1], (KP - 1,))
 
-        def later(g, pair, first_bank, slot=None):
-            acc = banks(pair, first_bank)
-            sums(g, list(pair), acc, range(KP))
-            hidden(g, pair, acc, False, slot)
+        quarter = S // 4
+        z = [product((n,), 0, quarter, n) for n in range(2)]
+        size = [keep.tile([P, quarter], F32, name=f"size{n}") for n in range(2)]
+        inv = [keep.tile([P, quarter], F32, name=f"inv{n}") for n in range(2)]
+        weighted = [keep.tile([P, quarter], F32, name=f"slot_first{n}", align_bytes=64) for n in range(2)]
+        y = [keep.tile([P, quarter], F32, name=f"y{n}") for n in range(2)]
+        for n in range(2):
+            nc.scalar.activation(size[n][:], z[n][:, 0, :], ACT.Abs)
+        for n in range(2):
+            nc.scalar.activation(inv[n][:], size[n][:], ACT.Abs_reciprocal_sqrt, bias=eps[:])
+            nc.vector.tensor_tensor(weighted[n][:], z[n][:, 0, :], weight[:, :quarter], MULT)
+        quantise_h(0, 2, 1, empty(0, (2,), accs[0], "relu_c")[:])
+        quantise_h(1, 2, 2, empty(1, (2, 3), accs[1], "relu_d")[:])
+        quantise_h(0, 3, 1, empty(0, (3,), accs[0], "relu_b", (True,))[:])
+        for n in range(2):
+            nc.vector.tensor_tensor(y[n][:], weighted[n][:], inv[n][:], MULT)
+        for n in range(2):
+            nc.vector.tensor_copy(cache[n][:].indirect(places[:, : quarter // 16]), y[n][:])
 
-        hidden(1, (2, 3), accs[1], False, "slot_gather", True)
-        hidden(0, (2, 3), accs[0], False, "slot_last")
-        project((0,), 0, 256, 0, "fused", "slot_first0")
-        project((1,), 0, 256, 1, "fused", "slot_first1")
-        later(0, (4, 5), 2, "slot_first0")
-        project((2,), 0, 256, 4, "fused")
-        later(1, (4, 5), 6, "slot_first1")
-        later(0, (6, 7), 0, "slot_late0")
-        later(1, (6, 7), 2, "slot_late1")
-        project((3,), 0, 256, 5, "vv", None, "slot_late0")
-        project((0,), 256, 256, 6, "vv", None, "slot_late1")
-        project((1, 2), 256, 256, 7, "gg", None, "slot_late1")
-        project((3,), 256, 512, 4, "gg", None, "slot_late1")
-        project((0, 1), 512, 256, 0, "gg", None, "slot_late1")
-        project((0, 1), 768, 256, 1, "gg", None, "slot_late1")
-        project((3,), 768, 256, 2, "gg", None, "slot_late1")
-        project((2,), 512, 512, 3, "gg", None, "slot_late1")
+        def later(pair, numbers, slots):
+            for g in range(HP):
+                acc = banks(pair, numbers[g])
+                sums(g, pair, acc, range(KP))
+                quantise_h(g, pair[0], 2, empty(g, pair, acc, slots[g])[:])
+
+        finish(*begin((2, 3), 0, quarter, 2, "slot_first1", "plain_first"))
+        item = begin((0, 1), quarter, quarter, 3, "slot_first1")
+        later((4, 5), ((4, 5), (6, 7)), ("relu_a", "slot_late0"))
+        finish(*item)
+        item = begin((2, 3), quarter, quarter, 2, "slot_late0")
+        later((6, 7), ((0, 1), (3, 4)), ("relu_b", "slot_late1"))
+        finish(*item, f"w1_codes{HP - 1}{KP - 1}")
+        finish(*begin((0, 1), 2 * quarter, quarter, 5, "slot_late1"))
+        finish(*begin((0, 1), 3 * quarter, quarter, 6, "slot_late1"))
+        finish(*begin((2,), half, half, 7, "slot_late1"))
+        finish(*begin((3,), half, half, 2, "slot_late1"))

@@ -43,39 +43,45 @@ def tile_list_descriptor_power_compression_kernel(tc, tab_words, tab_scales, w1,
         nc.gpsimd.memset(hundred[:], 100.0)
         nc.scalar.activation(eps[:], hundred[:], ACT.Abs_reciprocal_sqrt)
 
-        tab_sc = reuse.tile([P, KP, T // 4], I32, name="tab_sc", align_bytes=64, offset=8 * KB)
-        nc.vector.memset(tab_sc[:], 0)
+        tab_sc = [reuse.tile([P, T // 4], I32, name=f"tab_sc{a}", align_bytes=64, offset=(0, T, 4 * T - T // 2)[a]) for a in range(KP)]
+        for a in range(KP):
+            (nc.gpsimd if a == 1 else nc.vector).memset(tab_sc[a][:], 0)
         planes = keep.tile([P, KP * S // 4], I32, name="planes", align_bytes=64)
         nc.vector.memset(planes[:], 0)
+
+        tab = {0: reuse.tile([P, T], I32, name="tab0", align_bytes=64, offset=8 * T), 2: keep.tile([P, T], I32, name="tab2", align_bytes=64)}
+        words = [tab_words[a].rearrange("p t i -> p (t i)").bitcast(I32) for a in range(KP)]
+        raw = [keep.tile([P, PACK, H], F32, name=f"raw{a}") for a in range(KP - 1)]
+        rows = [w1[a * K_PASS : (a + 1) * K_PASS, :].rearrange("(p j) c -> p j c", j=PACK) for a in range(KP)]
+        nc.sync.dma_start(raw[0][:, 2, :K_PASS], rows[0][:, 2, :K_PASS])
+        nc.sync.dma_start(hits[:], offs)
+        nc.sync.dma_start(raw[0][:, 3, :K_PASS], rows[0][:, 3, :K_PASS])
+        nc.sync.dma_start(places[:], offs2)
+        for j in (0, 1):
+            nc.sync.dma_start(raw[0][:, j, :], rows[0][:, j, :])
+        for j in (2, 3):
+            nc.sync.dma_start(raw[0][:, j, K_PASS:], rows[0][:, j, K_PASS:])
+        for a in range(KP):
+            nc.sync.dma_start(tab_sc[a][0:P:8, :], tab_scales[a].bitcast(I32))
+        nc.sync.dma_start(tab[2][:], words[2])
+        nc.sync.dma_start(raw[1][:], rows[1])
+        nc.sync.dma_start(tab[0][:], words[0])
         cache = []
         for n in range(NT):
             window = keep.tile([P, T2], F32, name=f"cache{n}")
             nc.vector.memset(window[:], 0.0)
             cache.append(window)
 
-        tab = {0: keep.tile([P, T], I32, name="tab0", align_bytes=64), 1: reuse.tile([P, T], I32, name="tab1", align_bytes=64, offset=32 * KB)}
-        words = [tab_words[a].rearrange("p t i -> p (t i)").bitcast(I32) for a in range(KP)]
-        raw = [keep.tile([P, PACK, H], F32, name=f"raw{a}") for a in range(KP - 1)]
-        rows = [w1[a * K_PASS : (a + 1) * K_PASS, :].rearrange("(p j) c -> p j c", j=PACK) for a in range(KP)]
-        nc.sync.dma_start(raw[0][:], rows[0])
-        nc.sync.dma_start(hits[:], offs)
-        nc.sync.dma_start(tab_sc[0:P:8, :, :], tab_scales.rearrange("a r c -> r a c").bitcast(I32))
-        nc.sync.dma_start(places[:], offs2)
-        nc.sync.dma_start(tab[0][:], words[0])
-        nc.sync.dma_start(raw[1][:], rows[1])
-        nc.sync.dma_start(tab[1][:], words[1])
-
-        picked_sc = reuse.tile([P, KP * S], U8, name="picked_sc", align_bytes=64, offset=48 * KB)
+        picked_sc = reuse.tile([P, KP * S], U8, name="picked_sc", align_bytes=64, offset=7 * T - S)
         for a in range(KP):
-            nc.vector.tensor_copy(picked_sc[:, a * S : (a + 1) * S], tab_sc[:, a, :].bitcast(U8).indirect(hits[:]))
-        tab[2] = reuse.tile([P, T], I32, name="tab2", align_bytes=64, offset=0)
-        nc.sync.dma_start(tab[2][:, : T // 2], words[2][:, : T // 2])
+            nc.vector.tensor_copy(picked_sc[:, a * S : (a + 1) * S], tab_sc[a][:].bitcast(U8).indirect(hits[:]))
         for q in range(4):
             nc.sync.dma_start(planes[32 * q : 32 * q + 4, :], picked_sc[32 * q : 32 * q + 32 : 8, :].bitcast(I32))
-        nc.sync.dma_start(tab[2][:, T // 2 :], words[2][:, T // 2 :])
+        tab[1] = reuse.tile([P, T], I32, name="tab1", align_bytes=64, offset=0)
+        nc.sync.dma_start(tab[1][:], words[1])
         last = {}
         for c0, c1 in ((0, 512), (512, 768), (768, 1024)):
-            last[c0] = reuse.tile([P, PACK, c1 - c0], F32, name=f"last{c0}", offset=16 * KB + 16 * c0)
+            last[c0] = reuse.tile([P, PACK, c1 - c0], F32, name=f"last{c0}", offset=4 * T + 16 * c0)
             nc.sync.dma_start(last[c0][:], rows[2][:, :, c0:c1])
 
         v_sc = planes[:].bitcast(U8)
@@ -111,7 +117,7 @@ def tile_list_descriptor_power_compression_kernel(tc, tab_words, tab_scales, w1,
         for a in range(KP - 1):
             for g in range(HP):
                 prepare(g, a, (("v" if (g, a) == (1, 1) else "s", 0, P, raw[a][:, :, g * K_PASS : (g + 1) * K_PASS]),), False)
-        for a in (0, 1):
+        for a in (2, 0):
             for s in range(2):
                 gather(a, s)
         w2_sc = reuse.tile([P, HP * N // 4], I32, name="w2_sc", align_bytes=64, offset=32 * KB)
@@ -127,7 +133,7 @@ def tile_list_descriptor_power_compression_kernel(tc, tab_words, tab_scales, w1,
         nc.sync.dma_start(weight[:], wgo)
 
         for s in range(2):
-            gather(2, s)
+            gather(1, s)
         prepare(0, KP - 1, (("v", 0, 80, last[0][:, :, 0:320]), ("s", 80, P, last[0][:, :, 320:512])), True)
         prepare(1, KP - 1, (("s", 0, 64, last[512][:]), ("v", 64, P, last[768][:])), True)
 

@@ -137,7 +137,8 @@ def tile_list_descriptor_power_compression_kernel(tc, tab_words, tab_scales, w1,
         prepare(0, KP - 1, (("v", 0, 80, last[0][:, :, 0:320]), ("s", 80, P, last[0][:, :, 320:512])), True)
         prepare(1, KP - 1, (("s", 0, 64, last[512][:]), ("v", 64, P, last[768][:])), True)
 
-        h_codes = [keep.tile([P, S], U32, name=f"h_codes{g}", align_bytes=64) for g in range(HP)]
+        quarter = S // 4
+        h_codes = {}
         h_sc = [keep.tile([P, S], U8, name=f"h_sc{g}", align_bytes=64) for g in range(HP)]
         w2_sc_bytes = w2_sc[:].bitcast(U8)
 
@@ -156,9 +157,15 @@ def tile_list_descriptor_power_compression_kernel(tc, tab_words, tab_scales, w1,
                             stop=(a == KP - 1 and t == PACK - 1),
                         )
 
-        def quantise_h(g, b0, blocks, relu):
+        def h_words(g, c0, width):
+            s, c = divmod(c0, quarter)
+            return h_codes[g, s][:, c : c + width].bitcast(FP8X4)
+
+        def quantise_h(g, b0, blocks, relu, slot=None):
+            if b0 % 2 == 0:
+                h_codes[g, b0 // 2] = keep.tile([P, quarter], U32, name=slot or f"h_codes{g}{b0}", align_bytes=64)
             cols = slice(b0 * BLK, (b0 + blocks) * BLK)
-            nc.vector.quantize_mx(out=h_codes[g][:, cols].bitcast(FP8X4), scales=h_sc[g][:, cols], in_=relu.rearrange("p n t -> p (n t)"))
+            nc.vector.quantize_mx(out=h_words(g, b0 * BLK, blocks * BLK), scales=h_sc[g][:, cols], in_=relu.rearrange("p n t -> p (n t)"))
 
         def empty(g, pair, accs, slot, on_vector=(False, False)):
             relu = keep.tile([P, len(pair) * BLK, PACK], BF16, name=slot, align_bytes=64)
@@ -175,7 +182,7 @@ def tile_list_descriptor_power_compression_kernel(tc, tab_words, tab_scales, w1,
 
         def product(rows, tok0, width, bank):
             z = psum.tile([P, len(rows), width], F32, name=f"bank{bank}")
-            step = width if width == 512 else BLK
+            step = BLK
             for i, n in enumerate(rows):
                 for c0 in range(0, width, step):
                     cols = slice(tok0 + c0, tok0 + c0 + step)
@@ -184,7 +191,7 @@ def tile_list_descriptor_power_compression_kernel(tc, tab_words, tab_scales, w1,
                             out=z[:, i, c0 : c0 + step],
                             lhsT=w2_codes[:, g, n * (P // 2) : (n + 1) * (P // 2)].bitcast(U8).bitcast(FP4X4),
                             lhsT_scale=w2_sc_bytes[:, g * N + n * P : g * N + (n + 1) * P],
-                            rhs=h_codes[g][:, cols].bitcast(FP8X4),
+                            rhs=h_words(g, tok0 + c0, step),
                             rhs_scale=h_sc[g][:, cols],
                             start=(g == 0),
                             stop=(g == HP - 1),
@@ -202,7 +209,7 @@ def tile_list_descriptor_power_compression_kernel(tc, tab_words, tab_scales, w1,
             nc.gpsimd.tensor_tensor(weighted[:], plain[:], weight[:, tok0 : tok0 + width].unsqueeze(1).to_broadcast(shape), MULT)
             return rows, tok0, width, size, weighted
 
-        def finish(rows, tok0, width, size, weighted, inv_slot=None):
+        def finish(rows, tok0, width, size, weighted, inv_slot=None, between=()):
             shape = [P, len(rows), width]
             if inv_slot:
                 inv = keep.tile(shape, F32, name=inv_slot, align_bytes=64)
@@ -211,6 +218,8 @@ def tile_list_descriptor_power_compression_kernel(tc, tab_words, tab_scales, w1,
             nc.scalar.activation(inv[:], size[:], ACT.Abs_reciprocal_sqrt, bias=eps[:])
             y = ring.tile(shape, F32, name="y")
             nc.gpsimd.tensor_tensor(y[:], weighted[:], inv[:], MULT)
+            for job in between:
+                quantise_h(*job)
             for i, n in enumerate(rows):
                 nc.vector.tensor_copy(cache[n][:].indirect(places[:, tok0 // 16 : (tok0 + width) // 16]), y[:, i, :])
                 if tok0 + width == S:
@@ -230,7 +239,6 @@ def tile_list_descriptor_power_compression_kernel(tc, tab_words, tab_scales, w1,
             quantise_h(1, b, 1, relu[:, b * BLK : (b + 1) * BLK, :])
         sums(1, (2, 3), accs[1], (KP - 1,))
 
-        quarter = S // 4
         z = [product((n,), 0, quarter, n) for n in range(2)]
         size = [keep.tile([P, quarter], F32, name=f"size{n}") for n in range(2)]
         inv = [keep.tile([P, quarter], F32, name=f"inv{n}") for n in range(2)]
@@ -249,19 +257,19 @@ def tile_list_descriptor_power_compression_kernel(tc, tab_words, tab_scales, w1,
         for n in range(2):
             nc.vector.tensor_copy(cache[n][:].indirect(places[:, : quarter // 16]), y[n][:])
 
-        def later(pair, numbers, slots):
+        def later(pair, numbers, slots, code_slots):
+            jobs = []
             for g in range(HP):
                 acc = banks(pair, numbers[g])
                 sums(g, pair, acc, range(KP))
-                quantise_h(g, pair[0], 2, empty(g, pair, acc, slots[g])[:])
+                jobs.append((g, pair[0], 2, empty(g, pair, acc, slots[g])[:], code_slots[g]))
+            return jobs
 
         finish(*begin((2, 3), 0, quarter, 2, "slot_first1", "plain_first"))
         item = begin((0, 1), quarter, quarter, 3, "slot_first1")
-        later((4, 5), ((4, 5), (6, 7)), ("relu_a", "slot_late0"))
-        finish(*item)
+        finish(*item, "inv_b", later((4, 5), ((4, 5), (6, 7)), ("relu_a", "slot_late0"), ("inv_b", "slot_first1")))
         item = begin((2, 3), quarter, quarter, 2, "slot_late0")
-        later((6, 7), ((0, 1), (3, 4)), ("relu_b", "slot_late1"))
-        finish(*item, f"w1_codes{HP - 1}{KP - 1}")
+        finish(*item, f"w1_codes{HP - 1}{KP - 1}", later((6, 7), ((0, 1), (3, 4)), ("relu_b", "slot_late1"), (f"w1_codes{HP - 1}{KP - 1}", "slot_late0")))
         finish(*begin((0, 1), 2 * quarter, quarter, 5, "slot_late1"))
         finish(*begin((0, 1), 3 * quarter, quarter, 6, "slot_late1"))
         finish(*begin((2,), half, half, 7, "slot_late1"))

@@ -43,45 +43,38 @@ def tile_list_descriptor_power_compression_kernel(tc, tab_words, tab_scales, w1,
         nc.gpsimd.memset(hundred[:], 100.0)
         nc.scalar.activation(eps[:], hundred[:], ACT.Abs_reciprocal_sqrt)
 
-        tab_sc = [reuse.tile([P, T // 4], I32, name=f"tab_sc{a}", align_bytes=64, offset=(0, T, 4 * T - T // 2)[a]) for a in range(KP)]
-        for a in range(KP):
-            (nc.gpsimd if a == 1 else nc.vector).memset(tab_sc[a][:], 0)
+        tab_sc = reuse.tile([P, KP, T // 4], I32, name="tab_sc", align_bytes=64, offset=8 * KB)
+        nc.vector.memset(tab_sc[:], 0)
         planes = keep.tile([P, KP * S // 4], I32, name="planes", align_bytes=64)
         nc.vector.memset(planes[:], 0)
-
-        tab = {0: reuse.tile([P, T], I32, name="tab0", align_bytes=64, offset=8 * T), 2: keep.tile([P, T], I32, name="tab2", align_bytes=64)}
-        words = [tab_words[a].rearrange("p t i -> p (t i)").bitcast(I32) for a in range(KP)]
-        raw = [keep.tile([P, PACK, H], F32, name=f"raw{a}") for a in range(KP - 1)]
-        rows = [w1[a * K_PASS : (a + 1) * K_PASS, :].rearrange("(p j) c -> p j c", j=PACK) for a in range(KP)]
-        nc.sync.dma_start(raw[0][:, 2, :K_PASS], rows[0][:, 2, :K_PASS])
-        nc.sync.dma_start(hits[:], offs)
-        nc.sync.dma_start(raw[0][:, 3, :K_PASS], rows[0][:, 3, :K_PASS])
-        nc.sync.dma_start(places[:], offs2)
-        for j in (0, 1):
-            nc.sync.dma_start(raw[0][:, j, :], rows[0][:, j, :])
-        for j in (2, 3):
-            nc.sync.dma_start(raw[0][:, j, K_PASS:], rows[0][:, j, K_PASS:])
-        for a in range(KP):
-            nc.sync.dma_start(tab_sc[a][0:P:8, :], tab_scales[a].bitcast(I32))
-        nc.sync.dma_start(tab[2][:], words[2])
-        nc.sync.dma_start(raw[1][:], rows[1])
-        nc.sync.dma_start(tab[0][:], words[0])
         cache = []
         for n in range(NT):
             window = keep.tile([P, T2], F32, name=f"cache{n}")
             nc.vector.memset(window[:], 0.0)
             cache.append(window)
 
-        picked_sc = reuse.tile([P, KP * S], U8, name="picked_sc", align_bytes=64, offset=7 * T - S)
+        tab = {0: reuse.tile([P, T], I32, name="tab0", align_bytes=64, offset=32 * KB), 2: keep.tile([P, T], I32, name="tab2", align_bytes=64)}
+        words = [tab_words[a].rearrange("p t i -> p (t i)").bitcast(I32) for a in range(KP)]
+        raw = [keep.tile([P, PACK, H], F32, name=f"raw{a}") for a in range(KP - 1)]
+        rows = [w1[a * K_PASS : (a + 1) * K_PASS, :].rearrange("(p j) c -> p j c", j=PACK) for a in range(KP)]
+        nc.sync.dma_start(raw[0][:], rows[0])
+        nc.sync.dma_start(hits[:], offs)
+        nc.sync.dma_start(tab_sc[0:P:8, :, :], tab_scales.rearrange("a r c -> r a c").bitcast(I32))
+        nc.sync.dma_start(places[:], offs2)
+        nc.sync.dma_start(tab[2][:], words[2])
+        nc.sync.dma_start(raw[1][:], rows[1])
+        nc.sync.dma_start(tab[0][:], words[0])
+
+        picked_sc = reuse.tile([P, KP * S], U8, name="picked_sc", align_bytes=64, offset=48 * KB)
         for a in range(KP):
-            nc.vector.tensor_copy(picked_sc[:, a * S : (a + 1) * S], tab_sc[a][:].bitcast(U8).indirect(hits[:]))
+            nc.vector.tensor_copy(picked_sc[:, a * S : (a + 1) * S], tab_sc[:, a, :].bitcast(U8).indirect(hits[:]))
         for q in range(4):
             nc.sync.dma_start(planes[32 * q : 32 * q + 4, :], picked_sc[32 * q : 32 * q + 32 : 8, :].bitcast(I32))
         tab[1] = reuse.tile([P, T], I32, name="tab1", align_bytes=64, offset=0)
         nc.sync.dma_start(tab[1][:], words[1])
         last = {}
         for c0, c1 in ((0, 512), (512, 768), (768, 1024)):
-            last[c0] = reuse.tile([P, PACK, c1 - c0], F32, name=f"last{c0}", offset=4 * T + 16 * c0)
+            last[c0] = reuse.tile([P, PACK, c1 - c0], F32, name=f"last{c0}", offset=16 * KB + 16 * c0)
             nc.sync.dma_start(last[c0][:], rows[2][:, :, c0:c1])
 
         v_sc = planes[:].bitcast(U8)
@@ -120,10 +113,10 @@ def tile_list_descriptor_power_compression_kernel(tc, tab_words, tab_scales, w1,
         for a in (2, 0):
             for s in range(2):
                 gather(a, s)
-        w2_sc = reuse.tile([P, HP * N // 4], I32, name="w2_sc", align_bytes=64, offset=32 * KB)
-        nc.vector.memset(w2_sc[:], 0)
+        w2_sc = keep.tile([P, HP * N // 4], I32, name="w2_sc", align_bytes=64)
+        nc.gpsimd.memset(w2_sc[:], 0)
         for q in range(4):
-            nc.sync.dma_start(
+            nc.gpsimd.dma_start(
                 w2_sc[32 * q : 32 * q + 4, :].rearrange("r (a c) -> r a c", a=HP),
                 w2_scales[:, 4 * q : 4 * q + 4, :].rearrange("a r c -> r a c").bitcast(I32),
             )
@@ -183,18 +176,18 @@ def tile_list_descriptor_power_compression_kernel(tc, tab_words, tab_scales, w1,
         def product(rows, tok0, width, bank):
             z = psum.tile([P, len(rows), width], F32, name=f"bank{bank}")
             step = BLK
-            for i, n in enumerate(rows):
-                for c0 in range(0, width, step):
-                    cols = slice(tok0 + c0, tok0 + c0 + step)
-                    for g in range(HP):
+            for g in range(HP):
+                for i, n in enumerate(rows):
+                    for c0 in range(0, width, step):
+                        cols = slice(tok0 + c0, tok0 + c0 + step)
                         nc.tensor.matmul_mx(
                             out=z[:, i, c0 : c0 + step],
                             lhsT=w2_codes[:, g, n * (P // 2) : (n + 1) * (P // 2)].bitcast(U8).bitcast(FP4X4),
                             lhsT_scale=w2_sc_bytes[:, g * N + n * P : g * N + (n + 1) * P],
                             rhs=h_words(g, tok0 + c0, step),
                             rhs_scale=h_sc[g][:, cols],
-                            start=(g == 0),
-                            stop=(g == HP - 1),
+                            start=(g == 0 and i == 0 and c0 == 0),
+                            stop=(g == HP - 1 and i == len(rows) - 1 and c0 + step == width),
                         )
             return z
 

@@ -113,10 +113,10 @@ def tile_list_descriptor_power_compression_kernel(tc, tab_words, tab_scales, w1,
         for a in (2, 0):
             for s in range(2):
                 gather(a, s)
-        w2_sc = keep.tile([P, HP * N // 4], I32, name="w2_sc", align_bytes=64)
-        nc.gpsimd.memset(w2_sc[:], 0)
+        w2_sc = reuse.tile([P, HP * N // 4], I32, name="w2_sc", align_bytes=64, offset=32 * KB)
+        nc.vector.memset(w2_sc[:], 0)
         for q in range(4):
-            nc.gpsimd.dma_start(
+            nc.sync.dma_start(
                 w2_sc[32 * q : 32 * q + 4, :].rearrange("r (a c) -> r a c", a=HP),
                 w2_scales[:, 4 * q : 4 * q + 4, :].rearrange("a r c -> r a c").bitcast(I32),
             )
@@ -264,6 +264,6 @@ def tile_list_descriptor_power_compression_kernel(tc, tab_words, tab_scales, w1,
         item = begin((2, 3), quarter, quarter, 2, "slot_late0")
         finish(*item, f"w1_codes{HP - 1}{KP - 1}", later((6, 7), ((0, 1), (3, 4)), ("relu_b", "slot_late1"), (f"w1_codes{HP - 1}{KP - 1}", "slot_late0")))
         finish(*begin((0, 1), 2 * quarter, quarter, 5, "slot_late1"))
-        finish(*begin((0, 1), 3 * quarter, quarter, 6, "slot_late1"))
+        finish(*begin((0, 1), 3 * quarter, quarter, 6, "weighted_b"))
         finish(*begin((2,), half, half, 7, "slot_late1"))
-        finish(*begin((3,), half, half, 2, "slot_late1"))
+        finish(*begin((3,), half, half, 2, "weighted_b"))

@@ -86,11 +86,14 @@ def tile_list_descriptor_power_compression_kernel(tc, tab_words, tab_scales, w1,
             v_codes[a, s] = keep.tile([P, half], U32, name=f"v_codes{a}{s}", align_bytes=64)
             nc.vector.tensor_copy(v_codes[a, s][:], tab[a][:].bitcast(U32).indirect(hits[:, s * half // 16 : (s + 1) * half // 16]))
 
-        def prepare(g, a, cuts, by_slice):
+        def prepare(g, a, cuts, by_slice, offset=None):
             grouped = ring.tile([P, PACK, P, PACK], BF16, name="grouped", align_bytes=64, bufs=2)
             dst = grouped[:].rearrange("p (u e) m j -> p u m j e", e=2)
             codes = keep.tile([P, K_PASS], U32, name=f"w1_codes{g}{a}", align_bytes=64)
-            scales = keep.tile([P, K_PASS], U8, name=f"w1_sc{g}{a}", align_bytes=64)
+            if offset is None:
+                scales = keep.tile([P, K_PASS], U8, name=f"w1_sc{g}{a}", align_bytes=64)
+            else:
+                scales = reuse.tile([P, K_PASS], U8, name=f"w1_sc{g}{a}", align_bytes=64, offset=offset)
             for who, m0, m1, piece in cuts:
                 src = piece.rearrange("p j (m u e) -> p u m j e", u=2, e=2)
                 if who == "v":
@@ -107,12 +110,12 @@ def tile_list_descriptor_power_compression_kernel(tc, tab_words, tab_scales, w1,
             w1_codes[g, a] = codes
             w1_sc[g, a] = scales
 
-        for a in range(KP - 1):
-            for g in range(HP):
-                prepare(g, a, (("v" if (g, a) == (1, 1) else "s", 0, P, raw[a][:, :, g * K_PASS : (g + 1) * K_PASS]),), False)
+        for g, a in ((0, 0), (1, 0), (0, 1)):
+            prepare(g, a, (("s", 0, P, raw[a][:, :, g * K_PASS : (g + 1) * K_PASS]),), False)
         for a in (2, 0):
             for s in range(2):
                 gather(a, s)
+        prepare(1, 1, (("s", 0, P, raw[1][:, :, K_PASS:]),), False, 46 * KB)
         w2_sc = reuse.tile([P, HP * N // 4], I32, name="w2_sc", align_bytes=64, offset=32 * KB)
         nc.vector.memset(w2_sc[:], 0)
         for q in range(4):

@@ -52,6 +52,13 @@ def tile_list_descriptor_power_compression_kernel(tc, tab_words, tab_scales, w1,
             window = keep.tile([P, T2], F32, name=f"cache{n}")
             nc.vector.memset(window[:], 0.0)
             cache.append(window)
+        w2_sc = keep.tile([P, HP * N // 4], I32, name="w2_sc", align_bytes=64)
+        nc.vector.memset(w2_sc[:], 0)
+        for q in range(4):
+            nc.gpsimd.dma_start(
+                w2_sc[32 * q : 32 * q + 4, :].rearrange("r (a c) -> r a c", a=HP),
+                w2_scales[:, 4 * q : 4 * q + 4, :].rearrange("a r c -> r a c").bitcast(I32),
+            )
 
         tab = {0: reuse.tile([P, T], I32, name="tab0", align_bytes=64, offset=32 * KB), 2: keep.tile([P, T], I32, name="tab2", align_bytes=64)}
         words = [tab_words[a].rearrange("p t i -> p (t i)").bitcast(I32) for a in range(KP)]
@@ -98,6 +105,9 @@ def tile_list_descriptor_power_compression_kernel(tc, tab_words, tab_scales, w1,
                 src = piece.rearrange("p j (m u e) -> p u m j e", u=2, e=2)
                 if who == "v":
                     nc.vector.tensor_copy(dst[:, :, m0:m1], src)
+                elif who == "vv":
+                    for u in range(2):
+                        nc.vector.tensor_copy(dst[:, u, m0:m1], src[:, u])
                 else:
                     for u in range(2):
                         nc.scalar.copy(dst[:, u, m0:m1], src[:, u])
@@ -116,13 +126,6 @@ def tile_list_descriptor_power_compression_kernel(tc, tab_words, tab_scales, w1,
             for s in range(2):
                 gather(a, s)
         prepare(1, 1, (("s", 0, P, raw[1][:, :, K_PASS:]),), False, 46 * KB)
-        w2_sc = reuse.tile([P, HP * N // 4], I32, name="w2_sc", align_bytes=64, offset=32 * KB)
-        nc.vector.memset(w2_sc[:], 0)
-        for q in range(4):
-            nc.sync.dma_start(
-                w2_sc[32 * q : 32 * q + 4, :].rearrange("r (a c) -> r a c", a=HP),
-                w2_scales[:, 4 * q : 4 * q + 4, :].rearrange("a r c -> r a c").bitcast(I32),
-            )
         w2_codes = reuse.tile([P, HP, 2 * N // 4], I32, name="w2_codes", align_bytes=64, offset=36 * KB)
         nc.sync.dma_start(w2_codes[:], w2_words.rearrange("a p c -> p a c").bitcast(I32))
         weight = reuse.tile([P, S], F32, name="weight", offset=40 * KB)
@@ -130,8 +133,8 @@ def tile_list_descriptor_power_compression_kernel(tc, tab_words, tab_scales, w1,
 
         for s in range(2):
             gather(1, s)
-        prepare(0, KP - 1, (("v", 0, 80, last[0][:, :, 0:320]), ("s", 80, P, last[0][:, :, 320:512])), True)
-        prepare(1, KP - 1, (("s", 0, 64, last[512][:]), ("v", 64, P, last[768][:])), True)
+        prepare(0, KP - 1, (("vv", 0, 80, last[0][:, :, 0:320]), ("s", 80, P, last[0][:, :, 320:512])), True)
+        prepare(1, KP - 1, (("s", 0, 64, last[512][:]), ("vv", 64, P, last[768][:])), True)
 
         quarter = S // 4
         h_codes = {}
@@ -163,9 +166,16 @@ def tile_list_descriptor_power_compression_kernel(tc, tab_words, tab_scales, w1,
             cols = slice(b0 * BLK, (b0 + blocks) * BLK)
             nc.vector.quantize_mx(out=h_words(g, b0 * BLK, blocks * BLK), scales=h_sc[g][:, cols], in_=relu.rearrange("p n t -> p (n t)"))
 
-        def empty(g, pair, accs, slot, on_vector=(False, False)):
-            relu = keep.tile([P, len(pair) * BLK, PACK], BF16, name=slot, align_bytes=64)
+        def empty(g, pair, accs, slot, on_vector=(False, False), offset=None, only=None, relu=None):
+            if relu is not None:
+                pass
+            elif offset is None:
+                relu = keep.tile([P, len(pair) * BLK, PACK], BF16, name=slot, align_bytes=64)
+            else:
+                relu = reuse.tile([P, len(pair) * BLK, PACK], BF16, name=slot, align_bytes=64, offset=offset)
             for i, b in enumerate(pair):
+                if only is not None and i != only:
+                    continue
                 part = relu[:, i * BLK : (i + 1) * BLK, :]
                 if on_vector[i]:
                     nc.vector.tensor_scalar_max(part, accs[b][:].rearrange("p t n -> p n t"), 0.0)
@@ -205,17 +215,26 @@ def tile_list_descriptor_power_compression_kernel(tc, tab_words, tab_scales, w1,
             nc.gpsimd.tensor_tensor(weighted[:], plain[:], weight[:, tok0 : tok0 + width].unsqueeze(1).to_broadcast(shape), MULT)
             return rows, tok0, width, size, weighted
 
-        def finish(rows, tok0, width, size, weighted, inv_slot=None, between=()):
+        def finish(rows, tok0, width, size, weighted, inv_slot=None, between=(), by_row=False):
             shape = [P, len(rows), width]
-            if inv_slot:
-                inv = keep.tile(shape, F32, name=inv_slot, align_bytes=64)
-            else:
-                inv = ring.tile(shape, F32, name="inv", bufs=2)
-            nc.scalar.activation(inv[:], size[:], ACT.Abs_reciprocal_sqrt, bias=eps[:])
             y = ring.tile(shape, F32, name="y")
-            nc.gpsimd.tensor_tensor(y[:], weighted[:], inv[:], MULT)
-            for job in between:
-                quantise_h(*job)
+            if by_row:
+                for i in range(len(rows)):
+                    inv = keep.tile([P, width], F32, name=f"{inv_slot}{i}", align_bytes=64)
+                    nc.scalar.activation(inv[:], size[:, i, :], ACT.Abs_reciprocal_sqrt, bias=eps[:])
+                    nc.gpsimd.tensor_tensor(y[:, i, :], weighted[:, i, :], inv[:], MULT)
+            else:
+                if inv_slot:
+                    inv = keep.tile(shape, F32, name=inv_slot, align_bytes=64)
+                else:
+                    inv = ring.tile(shape, F32, name="inv", bufs=2)
+                nc.scalar.activation(inv[:], size[:], ACT.Abs_reciprocal_sqrt, bias=eps[:])
+                if between:
+                    between[1]()
+                nc.gpsimd.tensor_tensor(y[:], weighted[:], inv[:], MULT)
+            if between:
+                for job in between[0]:
+                    quantise_h(*job)
             for i, n in enumerate(rows):
                 nc.vector.tensor_copy(cache[n][:].indirect(places[:, tok0 // 16 : (tok0 + width) // 16]), y[:, i, :])
                 if tok0 + width == S:
@@ -227,13 +246,16 @@ def tile_list_descriptor_power_compression_kernel(tc, tab_words, tab_scales, w1,
                 for pair in ((0, 1), (2, 3)):
                     sums(g, pair, accs[g], (a,))
         sums(0, (0, 1), accs[0], (KP - 1,))
-        quantise_h(0, 0, 2, empty(0, (0, 1), accs[0], "relu_a")[:])
+        relu_a = empty(0, (0, 1), accs[0], "relu_a")
         sums(0, (2, 3), accs[0], (KP - 1,))
+        relu_c = empty(0, (2, 3), accs[0], "relu_c", (True, False), 28 * KB)
+        quantise_h(0, 0, 2, relu_a[:])
         sums(1, (0, 1), accs[1], (KP - 1,))
         relu = empty(1, (0, 1), accs[1], "relu_b", (False, True))
         for b in range(2):
             quantise_h(1, b, 1, relu[:, b * BLK : (b + 1) * BLK, :])
         sums(1, (2, 3), accs[1], (KP - 1,))
+        quantise_h(0, 2, 2, relu_c[:], "relu_b")
 
         z = [product((n,), 0, quarter, n) for n in range(2)]
         size = [keep.tile([P, quarter], F32, name=f"size{n}") for n in range(2)]
@@ -245,28 +267,27 @@ def tile_list_descriptor_power_compression_kernel(tc, tab_words, tab_scales, w1,
         for n in range(2):
             nc.scalar.activation(inv[n][:], size[n][:], ACT.Abs_reciprocal_sqrt, bias=eps[:])
             nc.vector.tensor_tensor(weighted[n][:], z[n][:, 0, :], weight[:, :quarter], MULT)
-        quantise_h(0, 2, 1, empty(0, (2,), accs[0], "relu_c")[:])
         quantise_h(1, 2, 2, empty(1, (2, 3), accs[1], "relu_d")[:])
-        quantise_h(0, 3, 1, empty(0, (3,), accs[0], "relu_b", (True,))[:])
         for n in range(2):
             nc.vector.tensor_tensor(y[n][:], weighted[n][:], inv[n][:], MULT)
         for n in range(2):
             nc.vector.tensor_copy(cache[n][:].indirect(places[:, : quarter // 16]), y[n][:])
 
-        def later(pair, numbers, slots, code_slots):
+        def later(pair, numbers, slots, code_slots, hold):
             jobs = []
             for g in range(HP):
                 acc = banks(pair, numbers[g])
                 sums(g, pair, acc, range(KP))
-                jobs.append((g, pair[0], 2, empty(g, pair, acc, slots[g])[:], code_slots[g]))
-            return jobs
+                relu = empty(g, pair, acc, slots[g], only=(0 if g and hold else None))
+                jobs.append((g, pair[0], 2, relu[:], code_slots[g]))
+            return jobs, lambda: empty(g, pair, acc, None, only=1, relu=relu) if hold else None
 
-        finish(*begin((2, 3), 0, quarter, 2, "slot_first1", "plain_first"))
-        item = begin((0, 1), quarter, quarter, 3, "slot_first1")
-        finish(*item, "inv_b", later((4, 5), ((4, 5), (6, 7)), ("relu_a", "slot_late0"), ("inv_b", "slot_first1")))
+        finish(*begin((2, 3), 0, quarter, 2, "slot_first1", "plain_first"), "inv_row", (), True)
+        item = begin((0, 1), quarter, quarter, 3, "inv_row0")
+        finish(*item, "inv_b", later((4, 5), ((4, 5), (6, 7)), ("relu_a", "slot_late0"), ("inv_b", "inv_row0"), True))
         item = begin((2, 3), quarter, quarter, 2, "slot_late0")
-        finish(*item, f"w1_codes{HP - 1}{KP - 1}", later((6, 7), ((0, 1), (3, 4)), ("relu_b", "slot_late1"), (f"w1_codes{HP - 1}{KP - 1}", "slot_late0")))
-        finish(*begin((0, 1), 2 * quarter, quarter, 5, "slot_late1"))
+        finish(*item, f"w1_codes{HP - 1}{KP - 1}", later((6, 7), ((0, 1), (3, 4)), ("relu_d", "slot_late1"), (f"w1_codes{HP - 1}{KP - 1}", "slot_late0"), True))
+        finish(*begin((0, 1), 2 * quarter, quarter, 5, "slot_late1"), "inv_late", (), True)
         finish(*begin((0, 1), 3 * quarter, quarter, 6, "weighted_b"))
         finish(*begin((2,), half, half, 7, "slot_late1"))
         finish(*begin((3,), half, half, 2, "weighted_b"))

@@ -66,7 +66,7 @@ def tile_list_descriptor_power_compression_kernel(tc, tab_words, tab_scales, w1,
         rows = [w1[a * K_PASS : (a + 1) * K_PASS, :].rearrange("(p j) c -> p j c", j=PACK) for a in range(KP)]
         nc.sync.dma_start(raw[0][:], rows[0])
         nc.sync.dma_start(hits[:], offs)
-        nc.sync.dma_start(tab_sc[0:P:8, :, :], tab_scales.rearrange("a r c -> r a c").bitcast(I32))
+        nc.sync.dma_start(tab_sc[4:P:8, :, :], tab_scales.rearrange("a r c -> r a c").bitcast(I32))
         nc.sync.dma_start(places[:], offs2)
         nc.sync.dma_start(tab[2][:], words[2])
         nc.sync.dma_start(raw[1][:], rows[1])
@@ -76,7 +76,7 @@ def tile_list_descriptor_power_compression_kernel(tc, tab_words, tab_scales, w1,
         for a in range(KP):
             nc.vector.tensor_copy(picked_sc[:, a * S : (a + 1) * S], tab_sc[:, a, :].bitcast(U8).indirect(hits[:]))
         for q in range(4):
-            nc.sync.dma_start(planes[32 * q : 32 * q + 4, :], picked_sc[32 * q : 32 * q + 32 : 8, :].bitcast(I32))
+            nc.sync.dma_start(planes[32 * q + 8 : 32 * q + 12, :], picked_sc[32 * q + 4 : 32 * q + 32 : 8, :].bitcast(I32))
         tab[1] = reuse.tile([P, T], I32, name="tab1", align_bytes=64, offset=0)
         nc.sync.dma_start(tab[1][:], words[1])
         last = {}
@@ -84,7 +84,7 @@ def tile_list_descriptor_power_compression_kernel(tc, tab_words, tab_scales, w1,
             last[c0] = reuse.tile([P, PACK, c1 - c0], F32, name=f"last{c0}", offset=16 * KB + 16 * c0)
             nc.sync.dma_start(last[c0][:], rows[2][:, :, c0:c1])
 
-        v_sc = planes[:].bitcast(U8)
+        v_sc = planes[8:P, :].bitcast(U8)
         v_codes = {}
         w1_codes = {}
         w1_sc = {}
@@ -287,7 +287,7 @@ def tile_list_descriptor_power_compression_kernel(tc, tab_words, tab_scales, w1,
         finish(*item, "inv_b", later((4, 5), ((4, 5), (6, 7)), ("relu_a", "slot_late0"), ("inv_b", "inv_row0"), True))
         item = begin((2, 3), quarter, quarter, 2, "slot_late0")
         finish(*item, f"w1_codes{HP - 1}{KP - 1}", later((6, 7), ((0, 1), (3, 4)), ("relu_d", "slot_late1"), (f"w1_codes{HP - 1}{KP - 1}", "slot_late0"), True))
-        finish(*begin((0, 1), 2 * quarter, quarter, 5, "slot_late1"), "inv_late", (), True)
+        finish(*begin((0, 1), 2 * quarter, quarter, 5, "slot_late1"))
         finish(*begin((0, 1), 3 * quarter, quarter, 6, "weighted_b"))
         finish(*begin((2,), half, half, 7, "slot_late1"))
         finish(*begin((3,), half, half, 2, "weighted_b"))

@@ -123,7 +123,7 @@ def tile_list_descriptor_power_compression_kernel(tc, tab_words, tab_scales, w1,
         for g, a in ((0, 0), (1, 0), (0, 1)):
             prepare(g, a, (("s", 0, P, raw[a][:, :, g * K_PASS : (g + 1) * K_PASS]),), False)
         for a in (2, 0):
-            for s in range(2):
+            for s in (1, 0):
                 gather(a, s)
         prepare(1, 1, (("s", 0, P, raw[1][:, :, K_PASS:]),), False, 46 * KB)
         w2_codes = reuse.tile([P, HP, 2 * N // 4], I32, name="w2_codes", align_bytes=64, offset=36 * KB)

@@ -54,10 +54,10 @@ def tile_list_descriptor_power_compression_kernel(tc, tab_words, tab_scales, w1,
             cache.append(window)
         w2_sc = keep.tile([P, HP * N // 4], I32, name="w2_sc", align_bytes=64)
         nc.vector.memset(w2_sc[:], 0)
-        for q in range(4):
+        for r in range(4):
             nc.gpsimd.dma_start(
-                w2_sc[32 * q : 32 * q + 4, :].rearrange("r (a c) -> r a c", a=HP),
-                w2_scales[:, 4 * q : 4 * q + 4, :].rearrange("a r c -> r a c").bitcast(I32),
+                w2_sc[r:P:32, :].rearrange("q (a c) -> q a c", a=HP),
+                w2_scales[:, r:16:4, :].rearrange("a q c -> q a c").bitcast(I32),
             )
 
         tab = {0: reuse.tile([P, T], I32, name="tab0", align_bytes=64, offset=32 * KB), 2: keep.tile([P, T], I32, name="tab2", align_bytes=64)}
@@ -66,7 +66,7 @@ def tile_list_descriptor_power_compression_kernel(tc, tab_words, tab_scales, w1,
         rows = [w1[a * K_PASS : (a + 1) * K_PASS, :].rearrange("(p j) c -> p j c", j=PACK) for a in range(KP)]
         nc.sync.dma_start(raw[0][:], rows[0])
         nc.sync.dma_start(hits[:], offs)
-        nc.sync.dma_start(tab_sc[4:P:8, :, :], tab_scales.rearrange("a r c -> r a c").bitcast(I32))
+        nc.sync.dma_start(tab_sc[32:96:4, :, :], tab_scales.rearrange("a r c -> r a c").bitcast(I32))
         nc.sync.dma_start(places[:], offs2)
         nc.sync.dma_start(tab[2][:], words[2])
         nc.sync.dma_start(raw[1][:], rows[1])
@@ -75,8 +75,8 @@ def tile_list_descriptor_power_compression_kernel(tc, tab_words, tab_scales, w1,
         picked_sc = reuse.tile([P, KP * S], U8, name="picked_sc", align_bytes=64, offset=48 * KB)
         for a in range(KP):
             nc.vector.tensor_copy(picked_sc[:, a * S : (a + 1) * S], tab_sc[:, a, :].bitcast(U8).indirect(hits[:]))
-        for q in range(4):
-            nc.sync.dma_start(planes[32 * q + 8 : 32 * q + 12, :], picked_sc[32 * q + 4 : 32 * q + 32 : 8, :].bitcast(I32))
+        for r in range(4):
+            nc.sync.dma_start(planes[8 + r : P : 32, :], picked_sc[32 + 4 * r : 96 : 16, :].bitcast(I32))
         tab[1] = reuse.tile([P, T], I32, name="tab1", align_bytes=64, offset=0)
         nc.sync.dma_start(tab[1][:], words[1])
         last = {}

@@ -45,8 +45,9 @@ def tile_list_descriptor_power_compression_kernel(tc, tab_words, tab_scales, w1,
 
         tab_sc = reuse.tile([P, KP, T // 4], I32, name="tab_sc", align_bytes=64, offset=8 * KB)
         nc.vector.memset(tab_sc[:], 0)
-        planes = keep.tile([P, KP * S // 4], I32, name="planes", align_bytes=64)
-        nc.vector.memset(planes[:], 0)
+        planes = [keep.tile([P, KP * half // 4], I32, name=f"planes{s}", align_bytes=64) for s in range(2)]
+        for s in range(2):
+            nc.vector.memset(planes[s][:], 0)
         cache = []
         for n in range(NT):
             window = keep.tile([P, T2], F32, name=f"cache{n}")
@@ -75,8 +76,16 @@ def tile_list_descriptor_power_compression_kernel(tc, tab_words, tab_scales, w1,
         picked_sc = reuse.tile([P, KP * S], U8, name="picked_sc", align_bytes=64, offset=48 * KB)
         for a in range(KP):
             nc.vector.tensor_copy(picked_sc[:, a * S : (a + 1) * S], tab_sc[:, a, :].bitcast(U8).indirect(hits[:]))
-        for r in range(4):
-            nc.sync.dma_start(planes[8 + r : P : 32, :], picked_sc[32 + 4 * r : 96 : 16, :].bitcast(I32))
+
+        def move_rows(s):
+            cols = slice(s * half // 4, (s + 1) * half // 4)
+            for r in range(4):
+                nc.sync.dma_start(
+                    planes[s][8 + r : P : 32, :].rearrange("q (a c) -> q a c", a=KP),
+                    picked_sc[32 + 4 * r : 96 : 16, :].bitcast(I32).rearrange("q (a c) -> q a c", a=KP)[:, :, cols],
+                )
+
+        move_rows(0)
         tab[1] = reuse.tile([P, T], I32, name="tab1", align_bytes=64, offset=0)
         nc.sync.dma_start(tab[1][:], words[1])
         last = {}
@@ -84,7 +93,7 @@ def tile_list_descriptor_power_compression_kernel(tc, tab_words, tab_scales, w1,
             last[c0] = reuse.tile([P, PACK, c1 - c0], F32, name=f"last{c0}", offset=16 * KB + 16 * c0)
             nc.sync.dma_start(last[c0][:], rows[2][:, :, c0:c1])
 
-        v_sc = planes[8:P, :].bitcast(U8)
+        v_sc = [planes[s][8:P, :].bitcast(U8) for s in range(2)]
         v_codes = {}
         w1_codes = {}
         w1_sc = {}
@@ -130,6 +139,7 @@ def tile_list_descriptor_power_compression_kernel(tc, tab_words, tab_scales, w1,
         nc.sync.dma_start(w2_codes[:], w2_words.rearrange("a p c -> p a c").bitcast(I32))
         weight = reuse.tile([P, S], F32, name="weight", offset=40 * KB)
         nc.sync.dma_start(weight[:], wgo)
+        move_rows(1)
 
         for s in range(2):
             gather(1, s)
@@ -141,7 +151,7 @@ def tile_list_descriptor_power_compression_kernel(tc, tab_words, tab_scales, w1,
         h_sc = [keep.tile([P, S], U8, name=f"h_sc{g}", align_bytes=64) for g in range(HP)]
         w2_sc_bytes = w2_sc[:].bitcast(U8)
 
-        def sums(g, pair, accs, passes):
+        def sums(g, pair, accs, passes, final=KP - 1):
             for a in passes:
                 for t in range(PACK):
                     for b in pair:
@@ -151,9 +161,9 @@ def tile_list_descriptor_power_compression_kernel(tc, tab_words, tab_scales, w1,
                             lhsT=w1_codes[g, a][:, t * P : (t + 1) * P].bitcast(FP8X4),
                             lhsT_scale=w1_sc[g, a][:, t * P : (t + 1) * P],
                             rhs=v_codes[a, s][:, c0 : c0 + BLK].bitcast(FP8X4),
-                            rhs_scale=v_sc[:, a * S + b * BLK : a * S + (b + 1) * BLK],
+                            rhs_scale=v_sc[s][:, a * half + c0 : a * half + c0 + BLK],
                             start=(a == 0 and t == 0),
-                            stop=(a == KP - 1 and t == PACK - 1),
+                            stop=(a == final and t == PACK - 1),
                         )
 
         def h_words(g, c0, width):
@@ -244,10 +254,11 @@ def tile_list_descriptor_power_compression_kernel(tc, tab_words, tab_scales, w1,
         for a in range(KP - 1):
             for g in range(HP):
                 for pair in ((0, 1), (2, 3)):
-                    sums(g, pair, accs[g], (a,))
+                    if (a, g, pair) != (1, 0, (2, 3)):
+                        sums(g, pair, accs[g], (a,))
         sums(0, (0, 1), accs[0], (KP - 1,))
         relu_a = empty(0, (0, 1), accs[0], "relu_a")
-        sums(0, (2, 3), accs[0], (KP - 1,))
+        sums(0, (2, 3), accs[0], (KP - 1, 1), 1)
         relu_c = empty(0, (2, 3), accs[0], "relu_c", (True, False), 28 * KB)
         quantise_h(0, 0, 2, relu_a[:])
         sums(1, (0, 1), accs[1], (KP - 1,))

@@ -47,14 +47,14 @@ def tile_list_descriptor_power_compression_kernel(tc, tab_words, tab_scales, w1,
         nc.vector.memset(tab_sc[:], 0)
         planes = [keep.tile([P, KP * half // 4], I32, name=f"planes{s}", align_bytes=64) for s in range(2)]
         for s in range(2):
-            nc.vector.memset(planes[s][:], 0)
+            nc.gpsimd.memset(planes[s][:], 0)
         cache = []
         for n in range(NT):
             window = keep.tile([P, T2], F32, name=f"cache{n}")
             nc.vector.memset(window[:], 0.0)
             cache.append(window)
         w2_sc = keep.tile([P, HP * N // 4], I32, name="w2_sc", align_bytes=64)
-        nc.vector.memset(w2_sc[:], 0)
+        nc.gpsimd.memset(w2_sc[:], 0)
         for r in range(4):
             nc.gpsimd.dma_start(
                 w2_sc[r:P:32, :].rearrange("q (a c) -> q a c", a=HP),
@@ -68,7 +68,6 @@ def tile_list_descriptor_power_compression_kernel(tc, tab_words, tab_scales, w1,
         nc.sync.dma_start(raw[0][:], rows[0])
         nc.sync.dma_start(hits[:], offs)
         nc.sync.dma_start(tab_sc[32:96:4, :, :], tab_scales.rearrange("a r c -> r a c").bitcast(I32))
-        nc.sync.dma_start(places[:], offs2)
         nc.sync.dma_start(tab[2][:], words[2])
         nc.sync.dma_start(raw[1][:], rows[1])
         nc.sync.dma_start(tab[0][:], words[0])
@@ -89,7 +88,7 @@ def tile_list_descriptor_power_compression_kernel(tc, tab_words, tab_scales, w1,
         tab[1] = reuse.tile([P, T], I32, name="tab1", align_bytes=64, offset=0)
         nc.sync.dma_start(tab[1][:], words[1])
         last = {}
-        for c0, c1 in ((0, 512), (512, 768), (768, 1024)):
+        for c0, c1 in ((0, 512), (512, 896), (896, 1024)):
             last[c0] = reuse.tile([P, PACK, c1 - c0], F32, name=f"last{c0}", offset=16 * KB + 16 * c0)
             nc.sync.dma_start(last[c0][:], rows[2][:, :, c0:c1])
 
@@ -102,6 +101,12 @@ def tile_list_descriptor_power_compression_kernel(tc, tab_words, tab_scales, w1,
             v_codes[a, s] = keep.tile([P, half], U32, name=f"v_codes{a}{s}", align_bytes=64)
             nc.vector.tensor_copy(v_codes[a, s][:], tab[a][:].bitcast(U32).indirect(hits[:, s * half // 16 : (s + 1) * half // 16]))
 
+        def gather_all(a):
+            picked = keep.tile([P, S], U32, name=f"v_codes{a}", align_bytes=64)
+            nc.vector.tensor_copy(picked[:], tab[a][:].bitcast(U32).indirect(hits[:]))
+            for s in range(2):
+                v_codes[a, s] = picked[:, s * half : (s + 1) * half]
+
         def prepare(g, a, cuts, by_slice, offset=None):
             grouped = ring.tile([P, PACK, P, PACK], BF16, name="grouped", align_bytes=64, bufs=2)
             dst = grouped[:].rearrange("p (u e) m j -> p u m j e", e=2)
@@ -111,6 +116,11 @@ def tile_list_descriptor_power_compression_kernel(tc, tab_words, tab_scales, w1,
             else:
                 scales = reuse.tile([P, K_PASS], U8, name=f"w1_sc{g}{a}", align_bytes=64, offset=offset)
             for who, m0, m1, piece in cuts:
+                if who == "q":
+                    for t in piece:
+                        cols = slice(t * P + m0, t * P + m1)
+                        nc.vector.quantize_mx(out=codes[:, cols].bitcast(FP8X4), scales=scales[:, cols], in_=grouped[:, t, m0:m1].rearrange("p m j -> p (m j)"))
+                    continue
                 src = piece.rearrange("p j (m u e) -> p u m j e", u=2, e=2)
                 if who == "v":
                     nc.vector.tensor_copy(dst[:, :, m0:m1], src)
@@ -121,30 +131,43 @@ def tile_list_descriptor_power_compression_kernel(tc, tab_words, tab_scales, w1,
                     for u in range(2):
                         nc.scalar.copy(dst[:, u, m0:m1], src[:, u])
             if by_slice:
-                for t in range(PACK):
-                    cols = slice(t * P, (t + 1) * P)
-                    nc.vector.quantize_mx(out=codes[:, cols].bitcast(FP8X4), scales=scales[:, cols], in_=grouped[:, t].rearrange("p m j -> p (m j)"))
-            else:
+                for t in (0, 2):
+                    cols = slice(t * P, (t + 2) * P)
+                    nc.vector.quantize_mx(out=codes[:, cols].bitcast(FP8X4), scales=scales[:, cols], in_=grouped[:, t : t + 2].rearrange("p t m j -> p (t m j)"))
+            elif by_slice is not None:
                 nc.vector.quantize_mx(out=codes[:].bitcast(FP8X4), scales=scales[:], in_=grouped[:].rearrange("p t m j -> p (t m j)"))
             w1_codes[g, a] = codes
             w1_sc[g, a] = scales
 
         for g, a in ((0, 0), (1, 0), (0, 1)):
             prepare(g, a, (("s", 0, P, raw[a][:, :, g * K_PASS : (g + 1) * K_PASS]),), False)
-        for a in (2, 0):
-            for s in (1, 0):
-                gather(a, s)
+        gather_all(2)
+        for s in range(2):
+            gather(0, s)
         prepare(1, 1, (("s", 0, P, raw[1][:, :, K_PASS:]),), False, 46 * KB)
         w2_codes = reuse.tile([P, HP, 2 * N // 4], I32, name="w2_codes", align_bytes=64, offset=36 * KB)
         nc.sync.dma_start(w2_codes[:], w2_words.rearrange("a p c -> p a c").bitcast(I32))
+        move_rows(1)
         weight = reuse.tile([P, S], F32, name="weight", offset=40 * KB)
         nc.sync.dma_start(weight[:], wgo)
-        move_rows(1)
+        nc.sync.dma_start(places[:], offs2)
 
         for s in range(2):
             gather(1, s)
         prepare(0, KP - 1, (("vv", 0, 80, last[0][:, :, 0:320]), ("s", 80, P, last[0][:, :, 320:512])), True)
-        prepare(1, KP - 1, (("s", 0, 64, last[512][:]), ("vv", 64, P, last[768][:])), True)
+        prepare(
+            1,
+            KP - 1,
+            (
+                ("vv", 0, 64, last[512][:, :, 0:256]),
+                ("s", 64, 96, last[512][:, :, 256:384]),
+                ("q", 0, 64, (0, 1)),
+                ("vv", 96, P, last[896][:]),
+                ("q", 0, 64, (2, 3)),
+                ("q", 64, P, range(PACK)),
+            ),
+            None,
+        )
 
         quarter = S // 4
         h_codes = {}
@@ -257,14 +280,20 @@ def tile_list_descriptor_power_compression_kernel(tc, tab_words, tab_scales, w1,
                     if (a, g, pair) != (1, 0, (2, 3)):
                         sums(g, pair, accs[g], (a,))
         sums(0, (0, 1), accs[0], (KP - 1,))
-        relu_a = empty(0, (0, 1), accs[0], "relu_a")
+        relu_a = empty(0, (0, 1), accs[0], "relu_first", offset=24 * KB)
         sums(0, (2, 3), accs[0], (KP - 1, 1), 1)
-        relu_c = empty(0, (2, 3), accs[0], "relu_c", (True, False), 28 * KB)
+        relu_c = empty(0, (2, 3), accs[0], "relu_c", (True, False), 30 * KB)
         quantise_h(0, 0, 2, relu_a[:])
         sums(1, (0, 1), accs[1], (KP - 1,))
-        relu = empty(1, (0, 1), accs[1], "relu_b", (False, True))
-        for b in range(2):
-            quantise_h(1, b, 1, relu[:, b * BLK : (b + 1) * BLK, :])
+        relu = keep.tile([P, 2 * BLK, PACK], BF16, name="relu_b", align_bytes=64)
+        h_codes[1, 0] = keep.tile([P, quarter], U32, name="h_codes10", align_bytes=64)
+        for c0 in (0, BLK // 2):
+            cols = slice(c0, c0 + BLK // 2)
+            nc.scalar.activation(relu[:, cols, :], accs[1][0][:, :, cols].rearrange("p t n -> p n t"), ACT.Relu)
+            nc.vector.tensor_scalar_max(relu[:, BLK + c0 : BLK + c0 + BLK // 2, :], accs[1][1][:, :, cols].rearrange("p t n -> p n t"), 0.0)
+        for c0 in (0, BLK, BLK // 2, BLK + BLK // 2):
+            cols = slice(c0, c0 + BLK // 2)
+            nc.vector.quantize_mx(out=h_words(1, c0, BLK // 2), scales=h_sc[1][:, cols], in_=relu[:, cols, :].rearrange("p n t -> p (n t)"))
         sums(1, (2, 3), accs[1], (KP - 1,))
         quantise_h(0, 2, 2, relu_c[:], "relu_b")
 

@@ -45,16 +45,15 @@ def tile_list_descriptor_power_compression_kernel(tc, tab_words, tab_scales, w1,
 
         tab_sc = reuse.tile([P, KP, T // 4], I32, name="tab_sc", align_bytes=64, offset=8 * KB)
         nc.vector.memset(tab_sc[:], 0)
-        planes = [keep.tile([P, KP * half // 4], I32, name=f"planes{s}", align_bytes=64) for s in range(2)]
-        for s in range(2):
-            nc.gpsimd.memset(planes[s][:], 0)
+        scale_rows = keep.tile([P, (KP * S + HP * N) // 4], I32, name="scale_rows", align_bytes=64)
+        planes = [scale_rows[:, s * KP * half // 4 : (s + 1) * KP * half // 4] for s in range(2)]
         cache = []
         for n in range(NT):
             window = keep.tile([P, T2], F32, name=f"cache{n}")
             nc.vector.memset(window[:], 0.0)
             cache.append(window)
-        w2_sc = keep.tile([P, HP * N // 4], I32, name="w2_sc", align_bytes=64)
-        nc.gpsimd.memset(w2_sc[:], 0)
+        nc.vector.memset(scale_rows[:], 0)
+        w2_sc = scale_rows[:, KP * S // 4 :]
         for r in range(4):
             nc.gpsimd.dma_start(
                 w2_sc[r:P:32, :].rearrange("q (a c) -> q a c", a=HP),
@@ -68,6 +67,7 @@ def tile_list_descriptor_power_compression_kernel(tc, tab_words, tab_scales, w1,
         nc.sync.dma_start(raw[0][:], rows[0])
         nc.sync.dma_start(hits[:], offs)
         nc.sync.dma_start(tab_sc[32:96:4, :, :], tab_scales.rearrange("a r c -> r a c").bitcast(I32))
+        nc.sync.dma_start(places[:], offs2)
         nc.sync.dma_start(tab[2][:], words[2])
         nc.sync.dma_start(raw[1][:], rows[1])
         nc.sync.dma_start(tab[0][:], words[0])
@@ -76,19 +76,19 @@ def tile_list_descriptor_power_compression_kernel(tc, tab_words, tab_scales, w1,
         for a in range(KP):
             nc.vector.tensor_copy(picked_sc[:, a * S : (a + 1) * S], tab_sc[:, a, :].bitcast(U8).indirect(hits[:]))
 
-        def move_rows(s):
+        def move_rows(s, queue):
             cols = slice(s * half // 4, (s + 1) * half // 4)
             for r in range(4):
-                nc.sync.dma_start(
+                queue.dma_start(
                     planes[s][8 + r : P : 32, :].rearrange("q (a c) -> q a c", a=KP),
                     picked_sc[32 + 4 * r : 96 : 16, :].bitcast(I32).rearrange("q (a c) -> q a c", a=KP)[:, :, cols],
                 )
 
-        move_rows(0)
+        move_rows(0, nc.scalar)
         tab[1] = reuse.tile([P, T], I32, name="tab1", align_bytes=64, offset=0)
         nc.sync.dma_start(tab[1][:], words[1])
         last = {}
-        for c0, c1 in ((0, 512), (512, 896), (896, 1024)):
+        for c0, c1 in ((0, 512), (512, 768), (768, 1024)):
             last[c0] = reuse.tile([P, PACK, c1 - c0], F32, name=f"last{c0}", offset=16 * KB + 16 * c0)
             nc.sync.dma_start(last[c0][:], rows[2][:, :, c0:c1])
 
@@ -141,33 +141,19 @@ def tile_list_descriptor_power_compression_kernel(tc, tab_words, tab_scales, w1,
 
         for g, a in ((0, 0), (1, 0), (0, 1)):
             prepare(g, a, (("s", 0, P, raw[a][:, :, g * K_PASS : (g + 1) * K_PASS]),), False)
-        gather_all(2)
-        for s in range(2):
-            gather(0, s)
+        for a in (2, 0):
+            gather_all(a)
         prepare(1, 1, (("s", 0, P, raw[1][:, :, K_PASS:]),), False, 46 * KB)
         w2_codes = reuse.tile([P, HP, 2 * N // 4], I32, name="w2_codes", align_bytes=64, offset=36 * KB)
         nc.sync.dma_start(w2_codes[:], w2_words.rearrange("a p c -> p a c").bitcast(I32))
-        move_rows(1)
         weight = reuse.tile([P, S], F32, name="weight", offset=40 * KB)
         nc.sync.dma_start(weight[:], wgo)
-        nc.sync.dma_start(places[:], offs2)
+        move_rows(1, nc.sync)
 
         for s in range(2):
             gather(1, s)
         prepare(0, KP - 1, (("vv", 0, 80, last[0][:, :, 0:320]), ("s", 80, P, last[0][:, :, 320:512])), True)
-        prepare(
-            1,
-            KP - 1,
-            (
-                ("vv", 0, 64, last[512][:, :, 0:256]),
-                ("s", 64, 96, last[512][:, :, 256:384]),
-                ("q", 0, 64, (0, 1)),
-                ("vv", 96, P, last[896][:]),
-                ("q", 0, 64, (2, 3)),
-                ("q", 64, P, range(PACK)),
-            ),
-            None,
-        )
+        prepare(1, KP - 1, (("s", 0, 64, last[512][:]), ("vv", 64, P, last[768][:]), *(("q", 0, P, (t,)) for t in range(PACK))), None)
 
         quarter = S // 4
         h_codes = {}
@@ -280,20 +266,14 @@ def tile_list_descriptor_power_compression_kernel(tc, tab_words, tab_scales, w1,
                     if (a, g, pair) != (1, 0, (2, 3)):
                         sums(g, pair, accs[g], (a,))
         sums(0, (0, 1), accs[0], (KP - 1,))
-        relu_a = empty(0, (0, 1), accs[0], "relu_first", offset=24 * KB)
+        relu_a = empty(0, (0, 1), accs[0], "relu_a")
         sums(0, (2, 3), accs[0], (KP - 1, 1), 1)
-        relu_c = empty(0, (2, 3), accs[0], "relu_c", (True, False), 30 * KB)
+        relu_c = empty(0, (2, 3), accs[0], "relu_c", (True, False), 28 * KB)
         quantise_h(0, 0, 2, relu_a[:])
         sums(1, (0, 1), accs[1], (KP - 1,))
-        relu = keep.tile([P, 2 * BLK, PACK], BF16, name="relu_b", align_bytes=64)
-        h_codes[1, 0] = keep.tile([P, quarter], U32, name="h_codes10", align_bytes=64)
-        for c0 in (0, BLK // 2):
-            cols = slice(c0, c0 + BLK // 2)
-            nc.scalar.activation(relu[:, cols, :], accs[1][0][:, :, cols].rearrange("p t n -> p n t"), ACT.Relu)
-            nc.vector.tensor_scalar_max(relu[:, BLK + c0 : BLK + c0 + BLK // 2, :], accs[1][1][:, :, cols].rearrange("p t n -> p n t"), 0.0)
-        for c0 in (0, BLK, BLK // 2, BLK + BLK // 2):
-            cols = slice(c0, c0 + BLK // 2)
-            nc.vector.quantize_mx(out=h_words(1, c0, BLK // 2), scales=h_sc[1][:, cols], in_=relu[:, cols, :].rearrange("p n t -> p (n t)"))
+        relu = empty(1, (0, 1), accs[1], "relu_b", (False, True))
+        for b in range(2):
+            quantise_h(1, b, 1, relu[:, b * BLK : (b + 1) * BLK, :])
         sums(1, (2, 3), accs[1], (KP - 1,))
         quantise_h(0, 2, 2, relu_c[:], "relu_b")
 

@@ -45,17 +45,18 @@ def tile_list_descriptor_power_compression_kernel(tc, tab_words, tab_scales, w1,
 
         tab_sc = reuse.tile([P, KP, T // 4], I32, name="tab_sc", align_bytes=64, offset=8 * KB)
         nc.vector.memset(tab_sc[:], 0)
+        nc.scalar.dma_start(tab_sc[32:96:4, :, :], tab_scales.rearrange("a r c -> r a c").bitcast(I32))
         scale_rows = keep.tile([P, (KP * S + HP * N) // 4], I32, name="scale_rows", align_bytes=64)
+        nc.vector.memset(scale_rows[:], 0)
         planes = [scale_rows[:, s * KP * half // 4 : (s + 1) * KP * half // 4] for s in range(2)]
         cache = []
         for n in range(NT):
             window = keep.tile([P, T2], F32, name=f"cache{n}")
             nc.vector.memset(window[:], 0.0)
             cache.append(window)
-        nc.vector.memset(scale_rows[:], 0)
         w2_sc = scale_rows[:, KP * S // 4 :]
         for r in range(4):
-            nc.gpsimd.dma_start(
+            nc.scalar.dma_start(
                 w2_sc[r:P:32, :].rearrange("q (a c) -> q a c", a=HP),
                 w2_scales[:, r:16:4, :].rearrange("a q c -> q a c").bitcast(I32),
             )
@@ -66,8 +67,6 @@ def tile_list_descriptor_power_compression_kernel(tc, tab_words, tab_scales, w1,
         rows = [w1[a * K_PASS : (a + 1) * K_PASS, :].rearrange("(p j) c -> p j c", j=PACK) for a in range(KP)]
         nc.sync.dma_start(raw[0][:], rows[0])
         nc.sync.dma_start(hits[:], offs)
-        nc.sync.dma_start(tab_sc[32:96:4, :, :], tab_scales.rearrange("a r c -> r a c").bitcast(I32))
-        nc.sync.dma_start(places[:], offs2)
         nc.sync.dma_start(tab[2][:], words[2])
         nc.sync.dma_start(raw[1][:], rows[1])
         nc.sync.dma_start(tab[0][:], words[0])
@@ -122,8 +121,8 @@ def tile_list_descriptor_power_compression_kernel(tc, tab_words, tab_scales, w1,
                         nc.vector.quantize_mx(out=codes[:, cols].bitcast(FP8X4), scales=scales[:, cols], in_=grouped[:, t, m0:m1].rearrange("p m j -> p (m j)"))
                     continue
                 src = piece.rearrange("p j (m u e) -> p u m j e", u=2, e=2)
-                if who == "v":
-                    nc.vector.tensor_copy(dst[:, :, m0:m1], src)
+                if who == "whole":
+                    nc.scalar.copy(dst[:, :, m0:m1], src)
                 elif who == "vv":
                     for u in range(2):
                         nc.vector.tensor_copy(dst[:, u, m0:m1], src[:, u])
@@ -140,12 +139,13 @@ def tile_list_descriptor_power_compression_kernel(tc, tab_words, tab_scales, w1,
             w1_sc[g, a] = scales
 
         for g, a in ((0, 0), (1, 0), (0, 1)):
-            prepare(g, a, (("s", 0, P, raw[a][:, :, g * K_PASS : (g + 1) * K_PASS]),), False)
+            prepare(g, a, (("whole", 0, P, raw[a][:, :, g * K_PASS : (g + 1) * K_PASS]),), False)
         for a in (2, 0):
             gather_all(a)
-        prepare(1, 1, (("s", 0, P, raw[1][:, :, K_PASS:]),), False, 46 * KB)
+        prepare(1, 1, (("whole", 0, P, raw[1][:, :, K_PASS:]),), False, 46 * KB)
         w2_codes = reuse.tile([P, HP, 2 * N // 4], I32, name="w2_codes", align_bytes=64, offset=36 * KB)
         nc.sync.dma_start(w2_codes[:], w2_words.rearrange("a p c -> p a c").bitcast(I32))
+        nc.sync.dma_start(places[:], offs2)
         weight = reuse.tile([P, S], F32, name="weight", offset=40 * KB)
         nc.sync.dma_start(weight[:], wgo)
         move_rows(1, nc.sync)

@@ -38,16 +38,14 @@ def tile_list_descriptor_power_compression_kernel(tc, tab_words, tab_scales, w1,
         hits = keep.tile([P, S // 16], U16, name="hits")
         places = keep.tile([P, S // 16], U16, name="places")
 
-        hundred = keep.tile([P, 1], F32, name="hundred")
-        eps = keep.tile([P, 1], F32, name="eps")
-        nc.gpsimd.memset(hundred[:], 100.0)
-        nc.scalar.activation(eps[:], hundred[:], ACT.Abs_reciprocal_sqrt)
-
         tab_sc = reuse.tile([P, KP, T // 4], I32, name="tab_sc", align_bytes=64, offset=8 * KB)
         nc.vector.memset(tab_sc[:], 0)
         nc.scalar.dma_start(tab_sc[32:96:4, :, :], tab_scales.rearrange("a r c -> r a c").bitcast(I32))
         scale_rows = keep.tile([P, (KP * S + HP * N) // 4], I32, name="scale_rows", align_bytes=64)
         nc.vector.memset(scale_rows[:], 0)
+        hundred = keep.tile([P, 1], F32, name="hundred")
+        eps = keep.tile([P, 1], F32, name="eps")
+        nc.vector.memset(hundred[:], 100.0)
         planes = [scale_rows[:, s * KP * half // 4 : (s + 1) * KP * half // 4] for s in range(2)]
         cache = []
         for n in range(NT):
@@ -60,6 +58,8 @@ def tile_list_descriptor_power_compression_kernel(tc, tab_words, tab_scales, w1,
                 w2_sc[r:P:32, :].rearrange("q (a c) -> q a c", a=HP),
                 w2_scales[:, r:16:4, :].rearrange("a q c -> q a c").bitcast(I32),
             )
+
+        nc.scalar.activation(eps[:], hundred[:], ACT.Abs_reciprocal_sqrt)
 
         tab = {0: reuse.tile([P, T], I32, name="tab0", align_bytes=64, offset=32 * KB), 2: keep.tile([P, T], I32, name="tab2", align_bytes=64)}
         words = [tab_words[a].rearrange("p t i -> p (t i)").bitcast(I32) for a in range(KP)]

@@ -96,15 +96,14 @@ def tile_list_descriptor_power_compression_kernel(tc, tab_words, tab_scales, w1,
         w1_codes = {}
         w1_sc = {}
 
-        def gather(a, s):
-            v_codes[a, s] = keep.tile([P, half], U32, name=f"v_codes{a}{s}", align_bytes=64)
-            nc.vector.tensor_copy(v_codes[a, s][:], tab[a][:].bitcast(U32).indirect(hits[:, s * half // 16 : (s + 1) * half // 16]))
-
-        def gather_all(a):
-            picked = keep.tile([P, S], U32, name=f"v_codes{a}", align_bytes=64)
-            nc.vector.tensor_copy(picked[:], tab[a][:].bitcast(U32).indirect(hits[:]))
-            for s in range(2):
-                v_codes[a, s] = picked[:, s * half : (s + 1) * half]
+        def gather(a, b0, blocks, offset=None):
+            if offset is None:
+                picked = keep.tile([P, blocks * BLK], U32, name=f"v_codes{a}{b0}", align_bytes=64)
+            else:
+                picked = reuse.tile([P, blocks * BLK], U32, name=f"v_codes{a}{b0}", align_bytes=64, offset=offset)
+            nc.vector.tensor_copy(picked[:], tab[a][:].bitcast(U32).indirect(hits[:, b0 * BLK // 16 : (b0 + blocks) * BLK // 16]))
+            for i in range(blocks):
+                v_codes[a, b0 + i] = picked[:, i * BLK : (i + 1) * BLK]
 
         def prepare(g, a, cuts, by_slice, offset=None):
             grouped = ring.tile([P, PACK, P, PACK], BF16, name="grouped", align_bytes=64, bufs=2)
@@ -141,7 +140,7 @@ def tile_list_descriptor_power_compression_kernel(tc, tab_words, tab_scales, w1,
         for g, a in ((0, 0), (1, 0), (0, 1)):
             prepare(g, a, (("whole", 0, P, raw[a][:, :, g * K_PASS : (g + 1) * K_PASS]),), False)
         for a in (2, 0):
-            gather_all(a)
+            gather(a, 0, 8)
         prepare(1, 1, (("whole", 0, P, raw[1][:, :, K_PASS:]),), False, 46 * KB)
         w2_codes = reuse.tile([P, HP, 2 * N // 4], I32, name="w2_codes", align_bytes=64, offset=36 * KB)
         nc.sync.dma_start(w2_codes[:], w2_words.rearrange("a p c -> p a c").bitcast(I32))
@@ -150,9 +149,10 @@ def tile_list_descriptor_power_compression_kernel(tc, tab_words, tab_scales, w1,
         nc.sync.dma_start(weight[:], wgo)
         move_rows(1, nc.sync)
 
-        for s in range(2):
-            gather(1, s)
+        gather(1, 0, 4)
+        gather(1, 4, 2)
         prepare(0, KP - 1, (("vv", 0, 80, last[0][:, :, 0:320]), ("s", 80, P, last[0][:, :, 320:512])), True)
+        gather(1, 6, 2, 16 * KB)
         prepare(1, KP - 1, (("s", 0, 64, last[512][:]), ("vv", 64, P, last[768][:]), *(("q", 0, P, (t,)) for t in range(PACK))), None)
 
         quarter = S // 4
@@ -169,7 +169,7 @@ def tile_list_descriptor_power_compression_kernel(tc, tab_words, tab_scales, w1,
                             out=accs[b][:, t, :],
                             lhsT=w1_codes[g, a][:, t * P : (t + 1) * P].bitcast(FP8X4),
                             lhsT_scale=w1_sc[g, a][:, t * P : (t + 1) * P],
-                            rhs=v_codes[a, s][:, c0 : c0 + BLK].bitcast(FP8X4),
+                            rhs=v_codes[a, b].bitcast(FP8X4),
                             rhs_scale=v_sc[s][:, a * half + c0 : a * half + c0 + BLK],
                             start=(a == 0 and t == 0),
                             stop=(a == final and t == PACK - 1),

@@ -151,7 +151,7 @@ def tile_list_descriptor_power_compression_kernel(tc, tab_words, tab_scales, w1,
 
         gather(1, 0, 4)
         gather(1, 4, 2)
-        prepare(0, KP - 1, (("vv", 0, 80, last[0][:, :, 0:320]), ("s", 80, P, last[0][:, :, 320:512])), True)
+        prepare(0, KP - 1, (("vv", 0, 88, last[0][:, :, 0:352]), ("s", 88, P, last[0][:, :, 352:512])), True)
         gather(1, 6, 2, 16 * KB)
         prepare(1, KP - 1, (("s", 0, 64, last[512][:]), ("vv", 64, P, last[768][:]), *(("q", 0, P, (t,)) for t in range(PACK))), None)
 

from contextlib import ExitStack

import concourse.mybir as mybir

K, H, N, T, S, T2 = 1536, 1024, 512, 4096, 1024, 2048
FLOPS = 2 * K * H * S + 2 * H * N * S

F32 = mybir.dt.float32
BF16 = mybir.dt.bfloat16
I32 = mybir.dt.int32
U32 = mybir.dt.uint32
U16 = mybir.dt.uint16
U8 = mybir.dt.uint8
FP8X4 = mybir.dt.float8_e4m3fn_x4
FP4X4 = mybir.dt.float4_e2m1fn_x4
ACT = mybir.ActivationFunctionType
MULT = mybir.AluOpType.mult

P = 128
PACK = 4
K_PASS = P * PACK
KP = K // K_PASS
HP = H // K_PASS
NT = N // P
BLK = 128


def tile_list_descriptor_power_compression_kernel(tc, tab_words, tab_scales, w1, w2_words, w2_scales, offs, offs2, wgo, out):
    nc = tc.nc
    with ExitStack() as ctx:
        keep = ctx.enter_context(tc.tile_pool(name="keep", bufs=1))
        ring = ctx.enter_context(tc.tile_pool(name="ring", bufs=3))
        reuse = ctx.enter_context(tc.tile_pool(name="reuse", bufs=1))
        psum = ctx.enter_context(tc.psum_pool(name="psum", bufs=1))
        KB = 1024
        half = S // 2

        hits = keep.tile([P, S // 16], U16, name="hits")
        places = keep.tile([P, S // 16], U16, name="places")

        tab_sc = reuse.tile([P, KP, T // 4], I32, name="tab_sc", align_bytes=64, offset=8 * KB)
        nc.vector.memset(tab_sc[:], 0)
        nc.scalar.dma_start(tab_sc[32:96:4, :, :], tab_scales.rearrange("a r c -> r a c").bitcast(I32))
        scale_rows = keep.tile([P, (KP * S + HP * N) // 4], I32, name="scale_rows", align_bytes=64)
        nc.vector.memset(scale_rows[:], 0)
        hundred = keep.tile([P, 1], F32, name="hundred")
        eps = keep.tile([P, 1], F32, name="eps")
        nc.vector.memset(hundred[:], 100.0)
        planes = [scale_rows[:, s * KP * half // 4 : (s + 1) * KP * half // 4] for s in range(2)]
        cache = []
        for n in range(NT):
            window = keep.tile([P, T2], F32, name=f"cache{n}")
            nc.vector.memset(window[:], 0.0)
            cache.append(window)
        w2_sc = scale_rows[:, KP * S // 4 :]
        for r in range(4):
            nc.scalar.dma_start(
                w2_sc[r:P:32, :].rearrange("q (a c) -> q a c", a=HP),
                w2_scales[:, r:16:4, :].rearrange("a q c -> q a c").bitcast(I32),
            )

        nc.scalar.activation(eps[:], hundred[:], ACT.Abs_reciprocal_sqrt)

        tab = {0: reuse.tile([P, T], I32, name="tab0", align_bytes=64, offset=32 * KB), 2: keep.tile([P, T], I32, name="tab2", align_bytes=64)}
        words = [tab_words[a].rearrange("p t i -> p (t i)").bitcast(I32) for a in range(KP)]
        raw = [keep.tile([P, PACK, H], F32, name=f"raw{a}") for a in range(KP - 1)]
        rows = [w1[a * K_PASS : (a + 1) * K_PASS, :].rearrange("(p j) c -> p j c", j=PACK) for a in range(KP)]
        nc.sync.dma_start(raw[0][:], rows[0])
        nc.sync.dma_start(hits[:], offs)
        nc.sync.dma_start(tab[2][:], words[2])
        nc.sync.dma_start(raw[1][:], rows[1])
        nc.sync.dma_start(tab[0][:], words[0])

        picked_sc = reuse.tile([P, KP * S], U8, name="picked_sc", align_bytes=64, offset=48 * KB)
        for a in range(KP):
            nc.vector.tensor_copy(picked_sc[:, a * S : (a + 1) * S], tab_sc[:, a, :].bitcast(U8).indirect(hits[:]))

        def move_rows(s, queue):
            cols = slice(s * half // 4, (s + 1) * half // 4)
            for r in range(4):
                queue.dma_start(
                    planes[s][8 + r : P : 32, :].rearrange("q (a c) -> q a c", a=KP),
                    picked_sc[32 + 4 * r : 96 : 16, :].bitcast(I32).rearrange("q (a c) -> q a c", a=KP)[:, :, cols],
                )

        move_rows(0, nc.scalar)
        tab[1] = reuse.tile([P, T], I32, name="tab1", align_bytes=64, offset=0)
        nc.sync.dma_start(tab[1][:], words[1])
        last = {}
        for c0, c1 in ((0, 512), (512, 768), (768, 1024)):
            last[c0] = reuse.tile([P, PACK, c1 - c0], F32, name=f"last{c0}", offset=16 * KB + 16 * c0)
            nc.sync.dma_start(last[c0][:], rows[2][:, :, c0:c1])

        v_sc = [planes[s][8:P, :].bitcast(U8) for s in range(2)]
        v_codes = {}
        w1_codes = {}
        w1_sc = {}

        def gather(a, b0, blocks, offset=None):
            if offset is None:
                picked = keep.tile([P, blocks * BLK], U32, name=f"v_codes{a}{b0}", align_bytes=64)
            else:
                picked = reuse.tile([P, blocks * BLK], U32, name=f"v_codes{a}{b0}", align_bytes=64, offset=offset)
            nc.vector.tensor_copy(picked[:], tab[a][:].bitcast(U32).indirect(hits[:, b0 * BLK // 16 : (b0 + blocks) * BLK // 16]))
            for i in range(blocks):
                v_codes[a, b0 + i] = picked[:, i * BLK : (i + 1) * BLK]

        def prepare(g, a, cuts, by_slice, offset=None):
            grouped = ring.tile([P, PACK, P, PACK], BF16, name="grouped", align_bytes=64, bufs=2)
            dst = grouped[:].rearrange("p (u e) m j -> p u m j e", e=2)
            codes = keep.tile([P, K_PASS], U32, name=f"w1_codes{g}{a}", align_bytes=64)
            if offset is None:
                scales = keep.tile([P, K_PASS], U8, name=f"w1_sc{g}{a}", align_bytes=64)
            else:
                scales = reuse.tile([P, K_PASS], U8, name=f"w1_sc{g}{a}", align_bytes=64, offset=offset)
            for who, m0, m1, piece in cuts:
                if who == "q":
                    for t in piece:
                        cols = slice(t * P + m0, t * P + m1)
                        nc.vector.quantize_mx(out=codes[:, cols].bitcast(FP8X4), scales=scales[:, cols], in_=grouped[:, t, m0:m1].rearrange("p m j -> p (m j)"))
                    continue
                src = piece.rearrange("p j (m u e) -> p u m j e", u=2, e=2)
                if who == "whole":
                    nc.scalar.copy(dst[:, :, m0:m1], src)
                elif who == "vv":
                    for u in range(2):
                        nc.vector.tensor_copy(dst[:, u, m0:m1], src[:, u])
                else:
                    for u in range(2):
                        nc.scalar.copy(dst[:, u, m0:m1], src[:, u])
            if by_slice:
                for t in (0, 2):
                    cols = slice(t * P, (t + 2) * P)
                    nc.vector.quantize_mx(out=codes[:, cols].bitcast(FP8X4), scales=scales[:, cols], in_=grouped[:, t : t + 2].rearrange("p t m j -> p (t m j)"))
            elif by_slice is not None:
                nc.vector.quantize_mx(out=codes[:].bitcast(FP8X4), scales=scales[:], in_=grouped[:].rearrange("p t m j -> p (t m j)"))
            w1_codes[g, a] = codes
            w1_sc[g, a] = scales

        for g, a in ((0, 0), (1, 0), (0, 1)):
            prepare(g, a, (("whole", 0, P, raw[a][:, :, g * K_PASS : (g + 1) * K_PASS]),), False)
        for a in (2, 0):
            gather(a, 0, 8)
        prepare(1, 1, (("whole", 0, P, raw[1][:, :, K_PASS:]),), False, 46 * KB)
        w2_codes = reuse.tile([P, HP, 2 * N // 4], I32, name="w2_codes", align_bytes=64, offset=36 * KB)
        nc.sync.dma_start(w2_codes[:], w2_words.rearrange("a p c -> p a c").bitcast(I32))
        nc.sync.dma_start(places[:], offs2)
        weight = reuse.tile([P, S], F32, name="weight", offset=40 * KB)
        nc.sync.dma_start(weight[:], wgo)
        move_rows(1, nc.sync)

        gather(1, 0, 4)
        gather(1, 4, 2)
        prepare(0, KP - 1, (("vv", 0, 88, last[0][:, :, 0:352]), ("s", 88, P, last[0][:, :, 352:512])), True)
        gather(1, 6, 2, 16 * KB)
        prepare(1, KP - 1, (("s", 0, 64, last[512][:]), ("vv", 64, P, last[768][:]), *(("q", 0, P, (t,)) for t in range(PACK))), None)

        quarter = S // 4
        h_codes = {}
        h_sc = [keep.tile([P, S], U8, name=f"h_sc{g}", align_bytes=64) for g in range(HP)]
        w2_sc_bytes = w2_sc[:].bitcast(U8)

        def sums(g, pair, accs, passes, final=KP - 1):
            for a in passes:
                for t in range(PACK):
                    for b in pair:
                        s, c0 = divmod(b * BLK, half)
                        nc.tensor.matmul_mx(
                            out=accs[b][:, t, :],
                            lhsT=w1_codes[g, a][:, t * P : (t + 1) * P].bitcast(FP8X4),
                            lhsT_scale=w1_sc[g, a][:, t * P : (t + 1) * P],
                            rhs=v_codes[a, b].bitcast(FP8X4),
                            rhs_scale=v_sc[s][:, a * half + c0 : a * half + c0 + BLK],
                            start=(a == 0 and t == 0),
                            stop=(a == final and t == PACK - 1),
                        )

        def h_words(g, c0, width):
            s, c = divmod(c0, quarter)
            return h_codes[g, s][:, c : c + width].bitcast(FP8X4)

        def quantise_h(g, b0, blocks, relu, slot=None):
            if b0 % 2 == 0:
                h_codes[g, b0 // 2] = keep.tile([P, quarter], U32, name=slot or f"h_codes{g}{b0}", align_bytes=64)
            cols = slice(b0 * BLK, (b0 + blocks) * BLK)
            nc.vector.quantize_mx(out=h_words(g, b0 * BLK, blocks * BLK), scales=h_sc[g][:, cols], in_=relu.rearrange("p n t -> p (n t)"))

        def empty(g, pair, accs, slot, on_vector=(False, False), offset=None, only=None, relu=None):
            if relu is not None:
                pass
            elif offset is None:
                relu = keep.tile([P, len(pair) * BLK, PACK], BF16, name=slot, align_bytes=64)
            else:
                relu = reuse.tile([P, len(pair) * BLK, PACK], BF16, name=slot, align_bytes=64, offset=offset)
            for i, b in enumerate(pair):
                if only is not None and i != only:
                    continue
                part = relu[:, i * BLK : (i + 1) * BLK, :]
                if on_vector[i]:
                    nc.vector.tensor_scalar_max(part, accs[b][:].rearrange("p t n -> p n t"), 0.0)
                else:
                    nc.scalar.activation(part, accs[b][:].rearrange("p t n -> p n t"), ACT.Relu)
            return relu

        def banks(blocks, numbers):
            return {b: psum.tile([P, PACK, BLK], F32, name=f"bank{i}") for b, i in zip(blocks, numbers)}

        def product(rows, tok0, width, bank):
            z = psum.tile([P, len(rows), width], F32, name=f"bank{bank}")
            step = BLK
            for g in range(HP):
                for i, n in enumerate(rows):
                    for c0 in range(0, width, step):
                        cols = slice(tok0 + c0, tok0 + c0 + step)
                        nc.tensor.matmul_mx(
                            out=z[:, i, c0 : c0 + step],
                            lhsT=w2_codes[:, g, n * (P // 2) : (n + 1) * (P // 2)].bitcast(U8).bitcast(FP4X4),
                            lhsT_scale=w2_sc_bytes[:, g * N + n * P : g * N + (n + 1) * P],
                            rhs=h_words(g, tok0 + c0, step),
                            rhs_scale=h_sc[g][:, cols],
                            start=(g == 0 and i == 0 and c0 == 0),
                            stop=(g == HP - 1 and i == len(rows) - 1 and c0 + step == width),
                        )
            return z

        def begin(rows, tok0, width, bank, slot, plain_slot="plain"):
            shape = [P, len(rows), width]
            z = product(rows, tok0, width, bank)
            plain = keep.tile(shape, F32, name=plain_slot)
            nc.scalar.copy(plain[:], z[:])
            size = ring.tile(shape, F32, name="size", bufs=1)
            nc.scalar.activation(size[:], z[:], ACT.Abs)
            weighted = keep.tile(shape, F32, name=slot, align_bytes=64)
            nc.gpsimd.tensor_tensor(weighted[:], plain[:], weight[:, tok0 : tok0 + width].unsqueeze(1).to_broadcast(shape), MULT)
            return rows, tok0, width, size, weighted

        def finish(rows, tok0, width, size, weighted, inv_slot=None, between=(), by_row=False):
            shape = [P, len(rows), width]
            y = ring.tile(shape, F32, name="y")
            if by_row:
                for i in range(len(rows)):
                    inv = keep.tile([P, width], F32, name=f"{inv_slot}{i}", align_bytes=64)
                    nc.scalar.activation(inv[:], size[:, i, :], ACT.Abs_reciprocal_sqrt, bias=eps[:])
                    nc.gpsimd.tensor_tensor(y[:, i, :], weighted[:, i, :], inv[:], MULT)
            else:
                if inv_slot:
                    inv = keep.tile(shape, F32, name=inv_slot, align_bytes=64)
                else:
                    inv = ring.tile(shape, F32, name="inv", bufs=2)
                nc.scalar.activation(inv[:], size[:], ACT.Abs_reciprocal_sqrt, bias=eps[:])
                if between:
                    between[1]()
                nc.gpsimd.tensor_tensor(y[:], weighted[:], inv[:], MULT)
            if between:
                for job in between[0]:
                    quantise_h(*job)
            for i, n in enumerate(rows):
                nc.vector.tensor_copy(cache[n][:].indirect(places[:, tok0 // 16 : (tok0 + width) // 16]), y[:, i, :])
                if tok0 + width == S:
                    nc.sync.dma_start(out[n * P : (n + 1) * P, :], cache[n][:])

        accs = [banks((0, 1, 2, 3), range(4 * g, 4 * g + 4)) for g in range(HP)]
        for a in range(KP - 1):
            for g in range(HP):
                for pair in ((0, 1), (2, 3)):
                    if (a, g, pair) != (1, 0, (2, 3)):
                        sums(g, pair, accs[g], (a,))
        sums(0, (0, 1), accs[0], (KP - 1,))
        relu_a = empty(0, (0, 1), accs[0], "relu_a")
        sums(0, (2, 3), accs[0], (KP - 1, 1), 1)
        relu_c = empty(0, (2, 3), accs[0], "relu_c", (True, False), 28 * KB)
        quantise_h(0, 0, 2, relu_a[:])
        sums(1, (0, 1), accs[1], (KP - 1,))
        relu = empty(1, (0, 1), accs[1], "relu_b", (False, True))
        for b in range(2):
            quantise_h(1, b, 1, relu[:, b * BLK : (b + 1) * BLK, :])
        sums(1, (2, 3), accs[1], (KP - 1,))
        quantise_h(0, 2, 2, relu_c[:], "relu_b")

        z = [product((n,), 0, quarter, n) for n in range(2)]
        size = [keep.tile([P, quarter], F32, name=f"size{n}") for n in range(2)]
        inv = [keep.tile([P, quarter], F32, name=f"inv{n}") for n in range(2)]
        weighted = [keep.tile([P, quarter], F32, name=f"slot_first{n}", align_bytes=64) for n in range(2)]
        y = [keep.tile([P, quarter], F32, name=f"y{n}") for n in range(2)]
        for n in range(2):
            nc.scalar.activation(size[n][:], z[n][:, 0, :], ACT.Abs)
        for n in range(2):
            nc.scalar.activation(inv[n][:], size[n][:], ACT.Abs_reciprocal_sqrt, bias=eps[:])
            nc.vector.tensor_tensor(weighted[n][:], z[n][:, 0, :], weight[:, :quarter], MULT)
        quantise_h(1, 2, 2, empty(1, (2, 3), accs[1], "relu_d")[:])
        for n in range(2):
            nc.vector.tensor_tensor(y[n][:], weighted[n][:], inv[n][:], MULT)
        for n in range(2):
            nc.vector.tensor_copy(cache[n][:].indirect(places[:, : quarter // 16]), y[n][:])

        def later(pair, numbers, slots, code_slots, hold):
            jobs = []
            for g in range(HP):
                acc = banks(pair, numbers[g])
                sums(g, pair, acc, range(KP))
                relu = empty(g, pair, acc, slots[g], only=(0 if g and hold else None))
                jobs.append((g, pair[0], 2, relu[:], code_slots[g]))
            return jobs, lambda: empty(g, pair, acc, None, only=1, relu=relu) if hold else None

        finish(*begin((2, 3), 0, quarter, 2, "slot_first1", "plain_first"), "inv_row", (), True)
        item = begin((0, 1), quarter, quarter, 3, "inv_row0")
        finish(*item, "inv_b", later((4, 5), ((4, 5), (6, 7)), ("relu_a", "slot_late0"), ("inv_b", "inv_row0"), True))
        item = begin((2, 3), quarter, quarter, 2, "slot_late0")
        finish(*item, f"w1_codes{HP - 1}{KP - 1}", later((6, 7), ((0, 1), (3, 4)), ("relu_d", "slot_late1"), (f"w1_codes{HP - 1}{KP - 1}", "slot_late0"), True))
        finish(*begin((0, 1), 2 * quarter, quarter, 5, "slot_late1"))
        finish(*begin((0, 1), 3 * quarter, quarter, 6, "weighted_b"))
        finish(*begin((2,), half, half, 7, "slot_late1"))
        finish(*begin((3,), half, half, 2, "weighted_b"))
